import numpy as np
import ml_dtypes


def mxq(x, axis, fmt="e4m3"):
    dtype, down = {"e4m3": (ml_dtypes.float8_e4m3fn, 7), "e5m2": (ml_dtypes.float8_e5m2, 14)}[fmt]
    v = np.moveaxis(np.asarray(x, np.float32).astype(ml_dtypes.bfloat16).astype(np.float64), axis, -1)
    blocks = v.reshape(v.shape[:-1] + (-1, 32))
    amax = np.abs(blocks).max(-1, keepdims=True)
    byte = np.maximum(np.where(amax > 0, np.frexp(amax)[1] - 1 + 127, 0) - down, 1)
    scale = np.exp2(byte - 127.0)
    codes = (blocks / scale).astype(np.float32).astype(dtype).astype(np.float64)
    return np.moveaxis((codes * scale).reshape(v.shape), -1, axis)


WIDE = False


def mx_kscale(k):
    if not WIDE:
        return np.ones(k)
    levels = np.array([10, -10, 5, -5, 0])
    if k % 512:
        return np.exp2(np.random.permutation(np.resize(levels, k // 32))).repeat(32)
    a = np.empty((k // 512, 16))
    for p in range(k // 512):
        a[p, :8] = np.random.permutation(np.resize(levels, 8))
        for g in range(8):
            far = levels[np.abs(levels - a[p, g]) >= 10]
            a[p, g + 8] = far[np.random.randint(len(far))]
    return np.exp2(a.ravel()).repeat(32)


def f64(x):
    return np.asarray(x).astype(np.float64)


def striped(idx):
    return np.tile(idx.reshape(-1, 16).T, (8, 1)).astype(np.uint16)


def unstriped(offs):
    return offs[:16].T.reshape(-1).astype(np.int64)


E2M1 = np.array([0.0, 0.5, 1.0, 1.5, 2.0, 3.0, 4.0, 6.0, -0.0, -0.5, -1.0, -1.5, -2.0, -3.0, -4.0, -6.0])


def pack_fp4(w):
    k, n = w.shape
    w = f64(np.asarray(w, np.float32).astype(ml_dtypes.bfloat16)).reshape(k // 32, 32, n)
    amax = np.abs(w).max(1)
    mant, ex = np.frexp(amax / 6.0)
    byte = np.clip(np.where(amax > 0, np.where(mant > 0.5, ex, ex - 1) + 127, 1), 1, 254)
    scaled = (w * np.exp2(127.0 - byte)[:, None, :]).reshape(k, n).astype(np.float32)
    c = np.ascontiguousarray(scaled.reshape(k // 512, 128, 4, n).transpose(0, 1, 3, 2)).astype(ml_dtypes.float4_e2m1fn).view(np.uint8) & 0xF
    words = (c[..., 0::2] | (c[..., 1::2] << 4)).reshape(k // 512, 128, 2 * n)
    return np.ascontiguousarray(words), np.ascontiguousarray(byte.astype(np.uint8).reshape(k // 512, 16, n))


def unpack_fp4(words, scales):
    g, _, n = scales.shape
    words = np.ascontiguousarray(words).reshape(g, 128, n, 2)
    nib = np.empty((g, 128, n, 4), np.uint8)
    nib[..., 0::2] = words & 0xF
    nib[..., 1::2] = words >> 4
    vals = E2M1[nib] * np.repeat(np.exp2(scales.astype(np.float64) - 127.0), 8, axis=1)[..., None]
    return vals.transpose(0, 1, 3, 2).reshape(g * 512, n)


K, T, S, N, U = 512, 2048, 1024, 256, 1024


def setup_inputs():
    n = np.random.standard_normal
    s = mx_kscale(K)[:, None]
    packed_w1 = pack_fp4(n((K, N)) / np.sqrt(K) / s)
    return {
        "xT": (n((K, T)) * s).astype(np.float32),
        "w1_words": packed_w1[0],
        "w1_scales": packed_w1[1],
        "scale": np.random.uniform(0.5, 1.5, (N, U)).astype(np.float32),
        "offs": striped(np.random.permutation(T)[:S]),
        "task": striped(np.random.permutation(U)[(U * np.random.uniform(0, 1, S) ** 4).astype(np.int64)]),
    }


def reference(xT, w1_words, w1_scales, scale, offs, task):
    xq = mxq(f64(xT)[:, unstriped(offs)], 0, "e4m3")
    y = unpack_fp4(w1_words, w1_scales).T @ xq
    g = f64(scale)[:, unstriped(task)]
    return y * g

@@ -1,0 +1,129 @@
+from contextlib import ExitStack
+
+import concourse.mybir as mybir
+
+K, T, S, N, U = 512, 2048, 1024, 256, 1024
+FLOPS = 2 * K * N * S
+
+F32 = mybir.dt.float32
+BF16 = mybir.dt.bfloat16
+I32 = mybir.dt.int32
+U32 = mybir.dt.uint32
+U16 = mybir.dt.uint16
+U8 = mybir.dt.uint8
+FP8X4 = mybir.dt.float8_e4m3fn_x4
+FP4X4 = mybir.dt.float4_e2m1fn_x4
+MULT = mybir.AluOpType.mult
+
+P = 128
+LANES = 16
+M_TILES = N // P
+PIECE = 256
+TASK_PIECE = 512
+CHUNKS = [[(1024, 1024), (1024, 512)], [(1024, 1024), (512, 0), (256, 0), (256, 64)]]
+
+
+def tile_picked_none_e_kernel(tc, xT, w1_words, w1_scales, scale, offs, task, out):
+    nc = tc.nc
+    with ExitStack() as ctx:
+        keep = ctx.enter_context(tc.tile_pool(name="keep", bufs=1))
+        psum = ctx.enter_context(tc.psum_pool(name="psum", bufs=1))
+
+        task_list = keep.tile([P, S // LANES], U16, name="task_list")
+        token_list = keep.tile([P, S // LANES], U16, name="token_list")
+        nc.sync.dma_start(task_list[:], task)
+        tables = []
+        for m in range(M_TILES):
+            table = keep.tile([P, U], F32, name=f"table{m}")
+            nc.sync.dma_start(table[:], scale[m * P : (m + 1) * P, :])
+            tables.append(table)
+        nc.sync.dma_start(token_list[:], offs)
+
+        w_codes = keep.tile([P, 2 * N], U8, name="w_codes", align_bytes=64)
+        w_plane = keep.tile([P, N], U8, name="w_plane", align_bytes=64)
+        nc.gpsimd.memset(w_plane[:].bitcast(I32), 0)
+        nc.gpsimd.dma_start(w_codes[:].bitcast(I32), w1_words[0].bitcast(I32))
+        for q in range(4):
+            nc.gpsimd.dma_start(w_plane[32 * q : 32 * q + 4, :].bitcast(I32), w1_scales[0, 4 * q : 4 * q + 4, :].bitcast(I32))
+
+        x_rows = xT.rearrange("(p u e) t -> u p e t", u=2, e=2)
+        raw = []
+        for u in range(2):
+            c0 = 0
+            for i, (width, on_scalar) in enumerate(CHUNKS[u]):
+                chunk = keep.tile([P, 2, width], F32, name=f"x{u}_{i}")
+                nc.sync.dma_start(chunk[:], x_rows[u][:, :, c0 : c0 + width])
+                raw.append((u, c0, width, on_scalar, chunk))
+                c0 = c0 + width
+
+        gains = keep.tile([P, M_TILES, S], F32, name="gains")
+        for m in range(M_TILES):
+            for j0 in range(0, S, TASK_PIECE):
+                nc.vector.tensor_copy(
+                    gains[:, m, j0 : j0 + TASK_PIECE],
+                    tables[m][:].indirect(task_list[:, j0 // LANES : (j0 + TASK_PIECE) // LANES]),
+                )
+
+        pairs = [keep.tile([P, T, 2], BF16, name=f"pairs{u}") for u in range(2)]
+        words = [pairs[u][:].rearrange("p t e -> p (t e)").bitcast(U32) for u in range(2)]
+        pieces = list(range(0, S, PIECE))
+        picked = [keep.tile([P, 2, PIECE], U32, name=f"picked{i}") for i in range(len(pieces))]
+        woven = [keep.tile([P, PIECE, 2], U32, name=f"woven{i}", align_bytes=64) for i in range(len(pieces))]
+
+        def gather(u, i):
+            j0 = pieces[i]
+            dst = picked[i][:, u, :]
+            nc.vector.tensor_copy(dst, words[u].indirect(token_list[:, j0 // LANES : (j0 + PIECE) // LANES]))
+
+        for u in range(2):
+            for uu, c0, width, on_scalar, chunk in raw:
+                if uu != u:
+                    continue
+                if on_scalar > 0:
+                    nc.scalar.copy(pairs[u][:, c0 : c0 + on_scalar, :], chunk[:, :, 0:on_scalar].rearrange("p e c -> p c e"))
+                if on_scalar < width:
+                    nc.vector.tensor_copy(pairs[u][:, c0 + on_scalar : c0 + width, :], chunk[:, :, on_scalar:width].rearrange("p e c -> p c e"))
+            if u == 0:
+                for i in range(len(pieces)):
+                    gather(0, i)
+
+        out_rows = out.rearrange("(m p) j -> p m j", p=P)
+        codes = [keep.tile([P, PIECE], U32, name=f"codes{i}", align_bytes=64) for i in range(len(pieces))]
+        planes = [keep.tile([P, PIECE], U8, name=f"plane{i}", align_bytes=64) for i in range(len(pieces))]
+        accs = [psum.tile([P, M_TILES, PIECE], F32, name=f"acc{i}") for i in range(len(pieces))]
+        results = [keep.tile([P, M_TILES, PIECE], F32, name=f"result{i}") for i in range(len(pieces))]
+
+        def fetch(i):
+            gather(1, i)
+            nc.scalar.copy(woven[i][:], picked[i][:].rearrange("p u n -> p n u"))
+
+        def multiply(i):
+            nc.vector.quantize_mx(
+                out=codes[i][:].bitcast(FP8X4),
+                scales=planes[i][:],
+                in_=woven[i][:].rearrange("p n u -> p (n u)").bitcast(BF16),
+            )
+            for m in range(M_TILES):
+                nc.tensor.matmul_mx(
+                    out=accs[i][:, m, :],
+                    lhsT=w_codes[:, 2 * P * m : 2 * P * (m + 1)].bitcast(FP4X4),
+                    lhsT_scale=w_plane[:, P * m : P * (m + 1)],
+                    rhs=codes[i][:].bitcast(FP8X4),
+                    rhs_scale=planes[i][:],
+                    start=True,
+                    stop=True,
+                )
+
+        def finish(i):
+            j0 = pieces[i]
+            nc.vector.tensor_tensor(results[i][:], accs[i][:], gains[:, :, j0 : j0 + PIECE], MULT)
+            nc.sync.dma_start(out_rows[:, :, j0 : j0 + PIECE], results[i][:])
+
+        count = len(pieces)
+        for step in range(count + 3):
+            if step < count:
+                fetch(step)
+            if 0 <= step - 2 < count:
+                multiply(step - 2)
+            if 0 <= step - 3 < count:
+                finish(step - 3)

@@ -20,7 +20,7 @@ LANES = 16
 M_TILES = N // P
 PIECE = 256
 TASK_PIECE = 512
-CHUNKS = [[(1024, 1024), (1024, 512)], [(1024, 1024), (512, 0), (256, 0), (256, 64)]]
+CHUNKS = [[(1024, 1024), (512, 0), (512, 192)], [(512, 512), (512, 512), (512, 256), (256, 0), (256, 64)]]
 
 
 def tile_picked_none_e_kernel(tc, xT, w1_words, w1_scales, scale, offs, task, out):
@@ -67,7 +67,7 @@ def tile_picked_none_e_kernel(tc, xT, w1_words, w1_scales, scale, offs, task, ou
         pairs = [keep.tile([P, T, 2], BF16, name=f"pairs{u}") for u in range(2)]
         words = [pairs[u][:].rearrange("p t e -> p (t e)").bitcast(U32) for u in range(2)]
         pieces = list(range(0, S, PIECE))
-        picked = [keep.tile([P, 2, PIECE], U32, name=f"picked{i}") for i in range(len(pieces))]
+        picked = [keep.tile([P, 2, PIECE], U32, name=f"picked{i}", tag=f"picked{i}") for i in range(len(pieces))]
         woven = [keep.tile([P, PIECE, 2], U32, name=f"woven{i}", align_bytes=64) for i in range(len(pieces))]
 
         def gather(u, i):
@@ -91,7 +91,6 @@ def tile_picked_none_e_kernel(tc, xT, w1_words, w1_scales, scale, offs, task, ou
         codes = [keep.tile([P, PIECE], U32, name=f"codes{i}", align_bytes=64) for i in range(len(pieces))]
         planes = [keep.tile([P, PIECE], U8, name=f"plane{i}", align_bytes=64) for i in range(len(pieces))]
         accs = [psum.tile([P, M_TILES, PIECE], F32, name=f"acc{i}") for i in range(len(pieces))]
-        results = [keep.tile([P, M_TILES, PIECE], F32, name=f"result{i}") for i in range(len(pieces))]
 
         def fetch(i):
             gather(1, i)
@@ -114,16 +113,18 @@ def tile_picked_none_e_kernel(tc, xT, w1_words, w1_scales, scale, offs, task, ou
                     stop=True,
                 )
 
-        def finish(i):
-            j0 = pieces[i]
-            nc.vector.tensor_tensor(results[i][:], accs[i][:], gains[:, :, j0 : j0 + PIECE], MULT)
-            nc.sync.dma_start(out_rows[:, :, j0 : j0 + PIECE], results[i][:])
-
         count = len(pieces)
-        for step in range(count + 3):
-            if step < count:
-                fetch(step)
-            if 0 <= step - 2 < count:
-                multiply(step - 2)
-            if 0 <= step - 3 < count:
-                finish(step - 3)
+        for i in range(count):
+            fetch(i)
+        for i in range(count):
+            multiply(i)
+        results = keep.tile([P, count, M_TILES, PIECE], F32, name="results", tag=f"picked{count - 1}")
+        for i in range(count - 1):
+            j0 = pieces[i]
+            nc.vector.tensor_tensor(results[:, i], accs[i][:], gains[:, :, j0 : j0 + PIECE], MULT)
+            nc.sync.dma_start(out_rows[:, :, j0 : j0 + PIECE], results[:, i])
+        i = count - 1
+        j0 = pieces[i]
+        for m, queue in enumerate((nc.sync, nc.scalar)):
+            nc.vector.tensor_tensor(results[:, i, m, :], accs[i][:, m, :], gains[:, m, j0 : j0 + PIECE], MULT)
+            queue.dma_start(out_rows[:, m, j0 : j0 + PIECE], results[:, i, m, :])

@@ -20,7 +20,7 @@ LANES = 16
 M_TILES = N // P
 PIECE = 256
 TASK_PIECE = 512
-CHUNKS = [[(1024, 1024), (512, 0), (512, 192)], [(512, 512), (512, 512), (512, 256), (256, 0), (256, 64)]]
+CHUNKS = [[(1024, 1024), (1024, 384)], [(1024, 832), (512, 128), (512, 176)]]
 
 
 def tile_picked_none_e_kernel(tc, xT, w1_words, w1_scales, scale, offs, task, out):
@@ -41,10 +41,6 @@ def tile_picked_none_e_kernel(tc, xT, w1_words, w1_scales, scale, offs, task, ou
 
         w_codes = keep.tile([P, 2 * N], U8, name="w_codes", align_bytes=64)
         w_plane = keep.tile([P, N], U8, name="w_plane", align_bytes=64)
-        nc.gpsimd.memset(w_plane[:].bitcast(I32), 0)
-        nc.gpsimd.dma_start(w_codes[:].bitcast(I32), w1_words[0].bitcast(I32))
-        for q in range(4):
-            nc.gpsimd.dma_start(w_plane[32 * q : 32 * q + 4, :].bitcast(I32), w1_scales[0, 4 * q : 4 * q + 4, :].bitcast(I32))
 
         x_rows = xT.rearrange("(p u e) t -> u p e t", u=2, e=2)
         raw = []
@@ -56,6 +52,11 @@ def tile_picked_none_e_kernel(tc, xT, w1_words, w1_scales, scale, offs, task, ou
                 raw.append((u, c0, width, on_scalar, chunk))
                 c0 = c0 + width
 
+        nc.vector.memset(w_plane[:].bitcast(I32), 0)
+        nc.sync.dma_start(w_codes[:].bitcast(I32), w1_words[0].bitcast(I32))
+        for q in range(4):
+            nc.sync.dma_start(w_plane[32 * q : 32 * q + 4, :].bitcast(I32), w1_scales[0, 4 * q : 4 * q + 4, :].bitcast(I32))
+
         gains = keep.tile([P, M_TILES, S], F32, name="gains")
         for m in range(M_TILES):
             for j0 in range(0, S, TASK_PIECE):
@@ -66,14 +67,14 @@ def tile_picked_none_e_kernel(tc, xT, w1_words, w1_scales, scale, offs, task, ou
 
         pairs = [keep.tile([P, T, 2], BF16, name=f"pairs{u}") for u in range(2)]
         words = [pairs[u][:].rearrange("p t e -> p (t e)").bitcast(U32) for u in range(2)]
-        pieces = list(range(0, S, PIECE))
-        picked = [keep.tile([P, 2, PIECE], U32, name=f"picked{i}", tag=f"picked{i}") for i in range(len(pieces))]
-        woven = [keep.tile([P, PIECE, 2], U32, name=f"woven{i}", align_bytes=64) for i in range(len(pieces))]
+        count = S // PIECE
+        slots = [(1, 2), (3, 4), (5, 6), (0, 2)]
+        picked = keep.tile([P, 7, PIECE], U32, name="picked", tag="staging")
+        woven = [keep.tile([P, PIECE, 2], U32, name=f"woven{i}", align_bytes=64) for i in range(count)]
 
         def gather(u, i):
-            j0 = pieces[i]
-            dst = picked[i][:, u, :]
-            nc.vector.tensor_copy(dst, words[u].indirect(token_list[:, j0 // LANES : (j0 + PIECE) // LANES]))
+            j0 = i * PIECE
+            nc.vector.tensor_copy(picked[:, slots[i][u], :], words[u].indirect(token_list[:, j0 // LANES : (j0 + PIECE) // LANES]))
 
         for u in range(2):
             for uu, c0, width, on_scalar, chunk in raw:
@@ -84,17 +85,17 @@ def tile_picked_none_e_kernel(tc, xT, w1_words, w1_scales, scale, offs, task, ou
                 if on_scalar < width:
                     nc.vector.tensor_copy(pairs[u][:, c0 + on_scalar : c0 + width, :], chunk[:, :, on_scalar:width].rearrange("p e c -> p c e"))
             if u == 0:
-                for i in range(len(pieces)):
+                for i in range(count):
                     gather(0, i)
 
-        out_rows = out.rearrange("(m p) j -> p m j", p=P)
-        codes = [keep.tile([P, PIECE], U32, name=f"codes{i}", align_bytes=64) for i in range(len(pieces))]
-        planes = [keep.tile([P, PIECE], U8, name=f"plane{i}", align_bytes=64) for i in range(len(pieces))]
-        accs = [psum.tile([P, M_TILES, PIECE], F32, name=f"acc{i}") for i in range(len(pieces))]
+        codes = [keep.tile([P, PIECE], U32, name=f"codes{i}", align_bytes=64) for i in range(count)]
+        planes = [keep.tile([P, PIECE], U8, name=f"plane{i}", align_bytes=64) for i in range(count)]
+        accs = [[psum.tile([P, 2 * PIECE], F32, name=f"acc{h}_{m}") for m in range(M_TILES)] for h in range(count // 2)]
 
         def fetch(i):
             gather(1, i)
-            nc.scalar.copy(woven[i][:], picked[i][:].rearrange("p u n -> p n u"))
+            first, second = slots[i]
+            nc.scalar.copy(woven[i][:], picked[:, first : second + 1 : second - first, :].rearrange("p u n -> p n u"))
 
         def multiply(i):
             nc.vector.quantize_mx(
@@ -104,7 +105,7 @@ def tile_picked_none_e_kernel(tc, xT, w1_words, w1_scales, scale, offs, task, ou
             )
             for m in range(M_TILES):
                 nc.tensor.matmul_mx(
-                    out=accs[i][:, m, :],
+                    out=accs[i // 2][m][:, (i % 2) * PIECE : (i % 2 + 1) * PIECE],
                     lhsT=w_codes[:, 2 * P * m : 2 * P * (m + 1)].bitcast(FP4X4),
                     lhsT_scale=w_plane[:, P * m : P * (m + 1)],
                     rhs=codes[i][:].bitcast(FP8X4),
@@ -113,18 +114,22 @@ def tile_picked_none_e_kernel(tc, xT, w1_words, w1_scales, scale, offs, task, ou
                     stop=True,
                 )
 
-        count = len(pieces)
-        for i in range(count):
-            fetch(i)
-        for i in range(count):
-            multiply(i)
-        results = keep.tile([P, count, M_TILES, PIECE], F32, name="results", tag=f"picked{count - 1}")
         for i in range(count - 1):
-            j0 = pieces[i]
-            nc.vector.tensor_tensor(results[:, i], accs[i][:], gains[:, :, j0 : j0 + PIECE], MULT)
-            nc.sync.dma_start(out_rows[:, :, j0 : j0 + PIECE], results[:, i])
-        i = count - 1
-        j0 = pieces[i]
-        for m, queue in enumerate((nc.sync, nc.scalar)):
-            nc.vector.tensor_tensor(results[:, i, m, :], accs[i][:, m, :], gains[:, m, j0 : j0 + PIECE], MULT)
-            queue.dma_start(out_rows[:, m, j0 : j0 + PIECE], results[:, i, m, :])
+            fetch(i)
+        multiply(0)
+        fetch(count - 1)
+        for i in range(1, count):
+            multiply(i)
+
+        results = keep.tile([P, M_TILES, S], F32, name="results", tag="staging")
+
+        def finish(m, j0, width, queue):
+            h, c0 = divmod(j0, 2 * PIECE)
+            nc.vector.tensor_tensor(results[:, m, j0 : j0 + width], accs[h][m][:, c0 : c0 + width], gains[:, m, j0 : j0 + width], MULT)
+            queue.dma_start(out[m * P : (m + 1) * P, j0 : j0 + width], results[:, m, j0 : j0 + width])
+
+        finish(0, 0, 2 * PIECE, nc.sync)
+        finish(1, 0, 2 * PIECE, nc.sync)
+        finish(0, 2 * PIECE, 2 * PIECE, nc.sync)
+        finish(1, 2 * PIECE, PIECE, nc.scalar)
+        finish(1, 3 * PIECE, PIECE, nc.sync)

@@ -20,7 +20,7 @@ LANES = 16
 M_TILES = N // P
 PIECE = 256
 TASK_PIECE = 512
-CHUNKS = [[(1024, 1024), (1024, 384)], [(1024, 832), (512, 128), (512, 176)]]
+CHUNKS = [[(1024, 1024), (1024, 384)], [(1024, 832), (768, 192), (256, 96)]]
 
 
 def tile_picked_none_e_kernel(tc, xT, w1_words, w1_scales, scale, offs, task, out):
@@ -69,8 +69,8 @@ def tile_picked_none_e_kernel(tc, xT, w1_words, w1_scales, scale, offs, task, ou
         words = [pairs[u][:].rearrange("p t e -> p (t e)").bitcast(U32) for u in range(2)]
         count = S // PIECE
         slots = [(1, 2), (3, 4), (5, 6), (0, 2)]
-        picked = keep.tile([P, 7, PIECE], U32, name="picked", tag="staging")
-        woven = [keep.tile([P, PIECE, 2], U32, name=f"woven{i}", align_bytes=64) for i in range(count)]
+        picked = keep.tile([P, 7, PIECE], U32, name="picked")
+        woven = [keep.tile([P, PIECE, 2], U32, name=f"woven{i}", align_bytes=64) for i in range(count - 1)]
 
         def gather(u, i):
             j0 = i * PIECE
@@ -88,9 +88,10 @@ def tile_picked_none_e_kernel(tc, xT, w1_words, w1_scales, scale, offs, task, ou
                 for i in range(count):
                     gather(0, i)
 
-        codes = [keep.tile([P, PIECE], U32, name=f"codes{i}", align_bytes=64) for i in range(count)]
+        codes = [keep.tile([P, PIECE], U32, name=f"codes{i}", tag=f"codes{i}", align_bytes=64) for i in range(count)]
         planes = [keep.tile([P, PIECE], U8, name=f"plane{i}", align_bytes=64) for i in range(count)]
-        accs = [[psum.tile([P, 2 * PIECE], F32, name=f"acc{h}_{m}") for m in range(M_TILES)] for h in range(count // 2)]
+        accs = [psum.tile([P, M_TILES, PIECE], F32, name=f"acc{i}") for i in range(count - 1)]
+        last = [psum.tile([P, PIECE], F32, name=f"last{m}") for m in range(M_TILES)]
 
         def fetch(i):
             gather(1, i)
@@ -105,7 +106,7 @@ def tile_picked_none_e_kernel(tc, xT, w1_words, w1_scales, scale, offs, task, ou
             )
             for m in range(M_TILES):
                 nc.tensor.matmul_mx(
-                    out=accs[i // 2][m][:, (i % 2) * PIECE : (i % 2 + 1) * PIECE],
+                    out=accs[i][:, m, :] if i < count - 1 else last[m][:],
                     lhsT=w_codes[:, 2 * P * m : 2 * P * (m + 1)].bitcast(FP4X4),
                     lhsT_scale=w_plane[:, P * m : P * (m + 1)],
                     rhs=codes[i][:].bitcast(FP8X4),
@@ -114,22 +115,24 @@ def tile_picked_none_e_kernel(tc, xT, w1_words, w1_scales, scale, offs, task, ou
                     stop=True,
                 )
 
+        out_rows = out.rearrange("(m p) j -> p m j", p=P)
+
+        def finish(i):
+            cols = slice(i * PIECE, (i + 1) * PIECE)
+            result = keep.tile([P, M_TILES, PIECE], F32, name=f"result{i}")
+            if i < count - 1:
+                nc.vector.tensor_tensor(result[:], accs[i][:], gains[:, :, cols], MULT)
+            else:
+                for m in range(M_TILES):
+                    nc.vector.tensor_tensor(result[:, m, :], last[m][:], gains[:, m, cols], MULT)
+            nc.sync.dma_start(out_rows[:, :, cols], result[:])
+
         for i in range(count - 1):
             fetch(i)
         multiply(0)
+        woven.append(keep.tile([P, PIECE, 2], U32, name="woven_last", tag="codes0", align_bytes=64))
         fetch(count - 1)
         for i in range(1, count):
             multiply(i)
-
-        results = keep.tile([P, M_TILES, S], F32, name="results", tag="staging")
-
-        def finish(m, j0, width, queue):
-            h, c0 = divmod(j0, 2 * PIECE)
-            nc.vector.tensor_tensor(results[:, m, j0 : j0 + width], accs[h][m][:, c0 : c0 + width], gains[:, m, j0 : j0 + width], MULT)
-            queue.dma_start(out[m * P : (m + 1) * P, j0 : j0 + width], results[:, m, j0 : j0 + width])
-
-        finish(0, 0, 2 * PIECE, nc.sync)
-        finish(1, 0, 2 * PIECE, nc.sync)
-        finish(0, 2 * PIECE, 2 * PIECE, nc.sync)
-        finish(1, 2 * PIECE, PIECE, nc.scalar)
-        finish(1, 3 * PIECE, PIECE, nc.sync)
+            finish(i - 1)
+        finish(count - 1)

@@ -14,13 +14,17 @@ U8 = mybir.dt.uint8
 FP8X4 = mybir.dt.float8_e4m3fn_x4
 FP4X4 = mybir.dt.float4_e2m1fn_x4
 MULT = mybir.AluOpType.mult
+COPY = mybir.ActivationFunctionType.Copy
 
 P = 128
 LANES = 16
 M_TILES = N // P
 PIECE = 256
+COUNT = S // PIECE
 TASK_PIECE = 512
-CHUNKS = [[(1024, 1024), (1024, 384)], [(1024, 832), (768, 192), (256, 96)]]
+EARLY_LOADS = [1024, 1024]
+PAIR_LOADS = [(1024, 0), (768, 320), (256, 96)]
+LATE_LOADS = [512, 512, 512, 512]
 
 
 def tile_picked_none_e_kernel(tc, xT, w1_words, w1_scales, scale, offs, task, out):
@@ -31,85 +35,94 @@ def tile_picked_none_e_kernel(tc, xT, w1_words, w1_scales, scale, offs, task, ou
 
         task_list = keep.tile([P, S // LANES], U16, name="task_list")
         token_list = keep.tile([P, S // LANES], U16, name="token_list")
-        nc.sync.dma_start(task_list[:], task)
-        tables = []
-        for m in range(M_TILES):
-            table = keep.tile([P, U], F32, name=f"table{m}")
-            nc.sync.dma_start(table[:], scale[m * P : (m + 1) * P, :])
-            tables.append(table)
-        nc.sync.dma_start(token_list[:], offs)
-
+        tables = [keep.tile([P, U], F32, name=f"table{m}") for m in range(M_TILES)]
         w_codes = keep.tile([P, 2 * N], U8, name="w_codes", align_bytes=64)
         w_plane = keep.tile([P, N], U8, name="w_plane", align_bytes=64)
+        x_rows = xT.rearrange("(p t) c -> p t c", t=4)
 
-        x_rows = xT.rearrange("(p u e) t -> u p e t", u=2, e=2)
-        raw = []
-        for u in range(2):
+        def load_row(t, widths):
+            chunks = []
             c0 = 0
-            for i, (width, on_scalar) in enumerate(CHUNKS[u]):
-                chunk = keep.tile([P, 2, width], F32, name=f"x{u}_{i}")
-                nc.sync.dma_start(chunk[:], x_rows[u][:, :, c0 : c0 + width])
-                raw.append((u, c0, width, on_scalar, chunk))
+            for i, width in enumerate(widths):
+                chunk = keep.tile([P, width], F32, name=f"x{t}_{i}")
+                nc.sync.dma_start(chunk[:], x_rows[:, t, c0 : c0 + width])
+                chunks.append((c0, width, chunk))
                 c0 = c0 + width
+            return chunks
 
+        nc.sync.dma_start(task_list[:], task)
+        nc.sync.dma_start(tables[0][:], scale[0:P, :])
+        early = load_row(2, EARLY_LOADS)
+        nc.sync.dma_start(token_list[:], offs)
+        nc.sync.dma_start(tables[1][:], scale[P : 2 * P, :])
+        pair_chunks = []
+        c0 = 0
+        for i, (width, on_scalar) in enumerate(PAIR_LOADS):
+            chunk = keep.tile([P, 2, width], F32, name=f"x01_{i}")
+            nc.sync.dma_start(chunk[:], x_rows[:, 0:2, c0 : c0 + width])
+            pair_chunks.append((c0, width, on_scalar, chunk))
+            c0 = c0 + width
+        late = load_row(3, LATE_LOADS)
         nc.vector.memset(w_plane[:].bitcast(I32), 0)
         nc.sync.dma_start(w_codes[:].bitcast(I32), w1_words[0].bitcast(I32))
         for q in range(4):
             nc.sync.dma_start(w_plane[32 * q : 32 * q + 4, :].bitcast(I32), w1_scales[0, 4 * q : 4 * q + 4, :].bitcast(I32))
 
+        def entries(lst, i):
+            return lst[:, i * PIECE // LANES : (i + 1) * PIECE // LANES]
+
         gains = keep.tile([P, M_TILES, S], F32, name="gains")
+        woven = [keep.tile([P, PIECE, 4], BF16, name=f"woven{i}", align_bytes=64) for i in range(COUNT)]
+
+        def single_row(t, chunks):
+            row = keep.tile([P, T], BF16, name=f"row{t}")
+            for c0, width, chunk in chunks:
+                nc.scalar.copy(row[:, c0 : c0 + width], chunk[:])
+            for i in range(COUNT):
+                nc.scalar.activation(woven[i][:, :, t], row[:].indirect(entries(token_list, i)), COPY)
+
         for m in range(M_TILES):
             for j0 in range(0, S, TASK_PIECE):
                 nc.vector.tensor_copy(
                     gains[:, m, j0 : j0 + TASK_PIECE],
                     tables[m][:].indirect(task_list[:, j0 // LANES : (j0 + TASK_PIECE) // LANES]),
                 )
+        single_row(2, early)
 
-        pairs = [keep.tile([P, T, 2], BF16, name=f"pairs{u}") for u in range(2)]
-        words = [pairs[u][:].rearrange("p t e -> p (t e)").bitcast(U32) for u in range(2)]
-        count = S // PIECE
-        slots = [(1, 2), (3, 4), (5, 6), (0, 2)]
-        picked = keep.tile([P, 7, PIECE], U32, name="picked")
-        woven = [keep.tile([P, PIECE, 2], U32, name=f"woven{i}", align_bytes=64) for i in range(count - 1)]
+        pairs = keep.tile([P, T, 2], BF16, name="pairs")
+        for c0, width, on_scalar, chunk in pair_chunks:
+            if on_scalar > 0:
+                nc.scalar.copy(pairs[:, c0 : c0 + on_scalar, :], chunk[:, :, 0:on_scalar].rearrange("p e c -> p c e"))
+            nc.vector.tensor_copy(pairs[:, c0 + on_scalar : c0 + width, :], chunk[:, :, on_scalar:width].rearrange("p e c -> p c e"))
+        pair_words = pairs[:].rearrange("p t e -> p (t e)").bitcast(U32)
+        for i in range(COUNT):
+            words = woven[i][:].rearrange("p n t -> p (n t)").bitcast(U32).rearrange("p (n u) -> p n u", u=2)
+            nc.vector.tensor_copy(words[:, :, 0], pair_words.indirect(entries(token_list, i)))
+        single_row(3, late)
 
-        def gather(u, i):
-            j0 = i * PIECE
-            nc.vector.tensor_copy(picked[:, slots[i][u], :], words[u].indirect(token_list[:, j0 // LANES : (j0 + PIECE) // LANES]))
-
-        for u in range(2):
-            for uu, c0, width, on_scalar, chunk in raw:
-                if uu != u:
-                    continue
-                if on_scalar > 0:
-                    nc.scalar.copy(pairs[u][:, c0 : c0 + on_scalar, :], chunk[:, :, 0:on_scalar].rearrange("p e c -> p c e"))
-                if on_scalar < width:
-                    nc.vector.tensor_copy(pairs[u][:, c0 + on_scalar : c0 + width, :], chunk[:, :, on_scalar:width].rearrange("p e c -> p c e"))
-            if u == 0:
-                for i in range(count):
-                    gather(0, i)
-
-        codes = [keep.tile([P, PIECE], U32, name=f"codes{i}", tag=f"codes{i}", align_bytes=64) for i in range(count)]
-        planes = [keep.tile([P, PIECE], U8, name=f"plane{i}", align_bytes=64) for i in range(count)]
-        accs = [psum.tile([P, M_TILES, PIECE], F32, name=f"acc{i}") for i in range(count - 1)]
-        last = [psum.tile([P, PIECE], F32, name=f"last{m}") for m in range(M_TILES)]
-
-        def fetch(i):
-            gather(1, i)
-            first, second = slots[i]
-            nc.scalar.copy(woven[i][:], picked[:, first : second + 1 : second - first, :].rearrange("p u n -> p n u"))
+        planes = [keep.tile([P, PIECE], U8, name=f"plane{i}", align_bytes=64) for i in range(COUNT)]
+        split = (0, COUNT - 1)
+        accs = []
+        for i in range(COUNT):
+            if i in split:
+                accs.append([psum.tile([P, PIECE], F32, name=f"acc{i}_{m}")[:] for m in range(M_TILES)])
+            else:
+                both = psum.tile([P, M_TILES, PIECE], F32, name=f"acc{i}")
+                accs.append([both[:, m, :] for m in range(M_TILES)] + [both[:]])
 
         def multiply(i):
+            codes = keep.tile([P, PIECE], U32, name=f"codes{i}", tag=f"codes{i % 2}", align_bytes=64)
             nc.vector.quantize_mx(
-                out=codes[i][:].bitcast(FP8X4),
+                out=codes[:].bitcast(FP8X4),
                 scales=planes[i][:],
-                in_=woven[i][:].rearrange("p n u -> p (n u)").bitcast(BF16),
+                in_=woven[i][:].rearrange("p n t -> p (n t)"),
             )
             for m in range(M_TILES):
                 nc.tensor.matmul_mx(
-                    out=accs[i][:, m, :] if i < count - 1 else last[m][:],
+                    out=accs[i][m],
                     lhsT=w_codes[:, 2 * P * m : 2 * P * (m + 1)].bitcast(FP4X4),
                     lhsT_scale=w_plane[:, P * m : P * (m + 1)],
-                    rhs=codes[i][:].bitcast(FP8X4),
+                    rhs=codes[:].bitcast(FP8X4),
                     rhs_scale=planes[i][:],
                     start=True,
                     stop=True,
@@ -120,19 +133,16 @@ def tile_picked_none_e_kernel(tc, xT, w1_words, w1_scales, scale, offs, task, ou
         def finish(i):
             cols = slice(i * PIECE, (i + 1) * PIECE)
             result = keep.tile([P, M_TILES, PIECE], F32, name=f"result{i}")
-            if i < count - 1:
-                nc.vector.tensor_tensor(result[:], accs[i][:], gains[:, :, cols], MULT)
-            else:
+            if i in split:
                 for m in range(M_TILES):
-                    nc.vector.tensor_tensor(result[:, m, :], last[m][:], gains[:, m, cols], MULT)
-            nc.sync.dma_start(out_rows[:, :, cols], result[:])
+                    nc.vector.tensor_tensor(result[:, m, :], accs[i][m], gains[:, m, cols], MULT)
+                    nc.sync.dma_start(out_rows[:, m, cols], result[:, m, :])
+            else:
+                nc.vector.tensor_tensor(result[:], accs[i][M_TILES], gains[:, :, cols], MULT)
+                nc.sync.dma_start(out_rows[:, :, cols], result[:])
 
-        for i in range(count - 1):
-            fetch(i)
         multiply(0)
-        woven.append(keep.tile([P, PIECE, 2], U32, name="woven_last", tag="codes0", align_bytes=64))
-        fetch(count - 1)
-        for i in range(1, count):
+        for i in range(1, COUNT):
             multiply(i)
             finish(i - 1)
-        finish(count - 1)
+        finish(COUNT - 1)

@@ -22,9 +22,11 @@ M_TILES = N // P
 PIECE = 256
 COUNT = S // PIECE
 TASK_PIECE = 512
-EARLY_LOADS = [1024, 1024]
-PAIR_LOADS = [(1024, 0), (768, 320), (256, 96)]
-LATE_LOADS = [512, 512, 512, 512]
+PAIR_LOADS = [(512, 512, 0), (768, 512, 0), (512, 192, 0), (256, 96, 0)]
+ROW2_LOADS = [(1024, 640, 384), (512, 320, 192), (512, 320, 192)]
+ROW3_LOADS = [(512, 0, 512), (512, 0, 0), (512, 0, 512), (512, 0, 256)]
+ROW2_ON_VECTOR = (0,)
+ROW3_ON_VECTOR = (0,)
 
 
 def tile_picked_none_e_kernel(tc, xT, w1_words, w1_scales, scale, offs, task, out):
@@ -40,46 +42,43 @@ def tile_picked_none_e_kernel(tc, xT, w1_words, w1_scales, scale, offs, task, ou
         w_plane = keep.tile([P, N], U8, name="w_plane", align_bytes=64)
         x_rows = xT.rearrange("(p t) c -> p t c", t=4)
 
-        def load_row(t, widths):
-            chunks = []
+        def load_row(t, loads):
+            raw = keep.tile([P, T], F32, name=f"raw{t}")
             c0 = 0
-            for i, width in enumerate(widths):
-                chunk = keep.tile([P, width], F32, name=f"x{t}_{i}")
-                nc.sync.dma_start(chunk[:], x_rows[:, t, c0 : c0 + width])
-                chunks.append((c0, width, chunk))
+            for width, on_scalar, on_gpsimd in loads:
+                nc.sync.dma_start(raw[:, c0 : c0 + width], x_rows[:, t, c0 : c0 + width])
                 c0 = c0 + width
-            return chunks
+            return raw
 
         nc.sync.dma_start(task_list[:], task)
-        nc.sync.dma_start(tables[0][:], scale[0:P, :])
-        early = load_row(2, EARLY_LOADS)
-        nc.sync.dma_start(token_list[:], offs)
-        nc.sync.dma_start(tables[1][:], scale[P : 2 * P, :])
+        for m in range(M_TILES):
+            nc.sync.dma_start(tables[m][:], scale[m * P : (m + 1) * P, :])
         pair_chunks = []
         c0 = 0
-        for i, (width, on_scalar) in enumerate(PAIR_LOADS):
+        for i, (width, on_scalar, on_gpsimd) in enumerate(PAIR_LOADS):
             chunk = keep.tile([P, 2, width], F32, name=f"x01_{i}")
             nc.sync.dma_start(chunk[:], x_rows[:, 0:2, c0 : c0 + width])
-            pair_chunks.append((c0, width, on_scalar, chunk))
+            pair_chunks.append(chunk)
             c0 = c0 + width
-        late = load_row(3, LATE_LOADS)
+            if i == 0:
+                nc.sync.dma_start(token_list[:], offs)
+        raw2 = load_row(2, ROW2_LOADS)
+        raw3 = load_row(3, ROW3_LOADS)
         nc.vector.memset(w_plane[:].bitcast(I32), 0)
         nc.sync.dma_start(w_codes[:].bitcast(I32), w1_words[0].bitcast(I32))
         for q in range(4):
             nc.sync.dma_start(w_plane[32 * q : 32 * q + 4, :].bitcast(I32), w1_scales[0, 4 * q : 4 * q + 4, :].bitcast(I32))
 
-        def entries(lst, i):
-            return lst[:, i * PIECE // LANES : (i + 1) * PIECE // LANES]
+        def entries(i):
+            return token_list[:, i * PIECE // LANES : (i + 1) * PIECE // LANES]
+
+        def shares(width, on_scalar, on_gpsimd):
+            cuts = [0, on_scalar, on_scalar + on_gpsimd, width]
+            calls = [nc.scalar.copy, nc.gpsimd.tensor_copy, nc.vector.tensor_copy]
+            return [(calls[e], cuts[e], cuts[e + 1]) for e in range(3) if cuts[e] < cuts[e + 1]]
 
         gains = keep.tile([P, M_TILES, S], F32, name="gains")
         woven = [keep.tile([P, PIECE, 4], BF16, name=f"woven{i}", align_bytes=64) for i in range(COUNT)]
-
-        def single_row(t, chunks):
-            row = keep.tile([P, T], BF16, name=f"row{t}")
-            for c0, width, chunk in chunks:
-                nc.scalar.copy(row[:, c0 : c0 + width], chunk[:])
-            for i in range(COUNT):
-                nc.scalar.activation(woven[i][:, :, t], row[:].indirect(entries(token_list, i)), COPY)
 
         for m in range(M_TILES):
             for j0 in range(0, S, TASK_PIECE):
@@ -87,18 +86,33 @@ def tile_picked_none_e_kernel(tc, xT, w1_words, w1_scales, scale, offs, task, ou
                     gains[:, m, j0 : j0 + TASK_PIECE],
                     tables[m][:].indirect(task_list[:, j0 // LANES : (j0 + TASK_PIECE) // LANES]),
                 )
-        single_row(2, early)
 
         pairs = keep.tile([P, T, 2], BF16, name="pairs")
-        for c0, width, on_scalar, chunk in pair_chunks:
-            if on_scalar > 0:
-                nc.scalar.copy(pairs[:, c0 : c0 + on_scalar, :], chunk[:, :, 0:on_scalar].rearrange("p e c -> p c e"))
-            nc.vector.tensor_copy(pairs[:, c0 + on_scalar : c0 + width, :], chunk[:, :, on_scalar:width].rearrange("p e c -> p c e"))
+        c0 = 0
+        for load, chunk in zip(PAIR_LOADS, pair_chunks):
+            for call, a, b in shares(*load):
+                call(pairs[:, c0 + a : c0 + b, :], chunk[:, :, a:b].rearrange("p e c -> p c e"))
+            c0 = c0 + load[0]
         pair_words = pairs[:].rearrange("p t e -> p (t e)").bitcast(U32)
         for i in range(COUNT):
             words = woven[i][:].rearrange("p n t -> p (n t)").bitcast(U32).rearrange("p (n u) -> p n u", u=2)
-            nc.vector.tensor_copy(words[:, :, 0], pair_words.indirect(entries(token_list, i)))
-        single_row(3, late)
+            nc.vector.tensor_copy(words[:, :, 0], pair_words.indirect(entries(i)))
+
+        def single_row(t, raw, loads, on_vector):
+            row = keep.tile([P, T], BF16, name=f"row{t}")
+            c0 = 0
+            for load in loads:
+                for call, a, b in shares(*load):
+                    call(row[:, c0 + a : c0 + b], raw[:, c0 + a : c0 + b])
+                c0 = c0 + load[0]
+            for i in range(COUNT):
+                if i in on_vector:
+                    nc.vector.tensor_copy(woven[i][:, :, t], raw[:].indirect(entries(i)))
+                else:
+                    nc.scalar.activation(woven[i][:, :, t], row[:].indirect(entries(i)), COPY)
+
+        single_row(2, raw2, ROW2_LOADS, ROW2_ON_VECTOR)
+        single_row(3, raw3, ROW3_LOADS, ROW3_ON_VECTOR)
 
         planes = [keep.tile([P, PIECE], U8, name=f"plane{i}", align_bytes=64) for i in range(COUNT)]
         split = (0, COUNT - 1)

@@ -23,8 +23,8 @@ PIECE = 256
 COUNT = S // PIECE
 TASK_PIECE = 512
 PAIR_LOADS = [(512, 512, 0), (768, 512, 0), (512, 192, 0), (256, 96, 0)]
-ROW2_LOADS = [(1024, 640, 384), (512, 320, 192), (512, 320, 192)]
-ROW3_LOADS = [(512, 0, 512), (512, 0, 0), (512, 0, 512), (512, 0, 256)]
+ROW2_LOADS = [(512, 512, 0), (512, 512, 0), (512, 512, 0), (512, 512, 0)]
+ROW3_LOADS = [(512, 0, 512), (512, 0, 512), (512, 0, 512), (512, 0, 0)]
 ROW2_ON_VECTOR = (0,)
 ROW3_ON_VECTOR = (0,)
 
@@ -72,9 +72,12 @@ def tile_picked_none_e_kernel(tc, xT, w1_words, w1_scales, scale, offs, task, ou
         def entries(i):
             return token_list[:, i * PIECE // LANES : (i + 1) * PIECE // LANES]
 
+        def gpsimd_cast(dst, src):
+            nc.gpsimd.tensor_scalar(dst, src, 1.0, 0.0, MULT, mybir.AluOpType.add)
+
         def shares(width, on_scalar, on_gpsimd):
             cuts = [0, on_scalar, on_scalar + on_gpsimd, width]
-            calls = [nc.scalar.copy, nc.gpsimd.tensor_copy, nc.vector.tensor_copy]
+            calls = [nc.scalar.copy, gpsimd_cast, nc.vector.tensor_copy]
             return [(calls[e], cuts[e], cuts[e + 1]) for e in range(3) if cuts[e] < cuts[e + 1]]
 
         gains = keep.tile([P, M_TILES, S], F32, name="gains")

@@ -22,9 +22,9 @@ M_TILES = N // P
 PIECE = 256
 COUNT = S // PIECE
 TASK_PIECE = 512
-PAIR_LOADS = [(512, 512, 0), (768, 512, 0), (512, 192, 0), (256, 96, 0)]
-ROW2_LOADS = [(512, 512, 0), (512, 512, 0), (512, 512, 0), (512, 512, 0)]
-ROW3_LOADS = [(512, 0, 512), (512, 0, 512), (512, 0, 512), (512, 0, 0)]
+PAIR_LOADS = [(1024, 544, 480), (768, 288, 0), (256, 96, 0)]
+ROW2_LOADS = [(1024, 576, 448), (512, 256, 256), (512, 512, 0)]
+ROW3_LOADS = [(1024, 0, 1024), (512, 0, 0), (512, 0, 0)]
 ROW2_ON_VECTOR = (0,)
 ROW3_ON_VECTOR = (0,)
 

@@ -14,19 +14,23 @@ U8 = mybir.dt.uint8
 FP8X4 = mybir.dt.float8_e4m3fn_x4
 FP4X4 = mybir.dt.float4_e2m1fn_x4
 MULT = mybir.AluOpType.mult
+ADD = mybir.AluOpType.add
 COPY = mybir.ActivationFunctionType.Copy
 
 P = 128
+PACK = 4
 LANES = 16
 M_TILES = N // P
 PIECE = 256
 COUNT = S // PIECE
 TASK_PIECE = 512
+CODE_BUFFERS = 2
+
 PAIR_LOADS = [(1024, 544, 480), (768, 288, 0), (256, 96, 0)]
 ROW2_LOADS = [(1024, 576, 448), (512, 256, 256), (512, 512, 0)]
-ROW3_LOADS = [(1024, 0, 1024), (512, 0, 0), (512, 0, 0)]
-ROW2_ON_VECTOR = (0,)
-ROW3_ON_VECTOR = (0,)
+ROW3_LOADS = [(1024, 0, 1024), (1024, 0, 0)]
+VECTOR_PIECE = 0
+BY_BLOCK = (0, COUNT - 2, COUNT - 1)
 
 
 def tile_picked_none_e_kernel(tc, xT, w1_words, w1_scales, scale, offs, task, out):
@@ -40,14 +44,14 @@ def tile_picked_none_e_kernel(tc, xT, w1_words, w1_scales, scale, offs, task, ou
         tables = [keep.tile([P, U], F32, name=f"table{m}") for m in range(M_TILES)]
         w_codes = keep.tile([P, 2 * N], U8, name="w_codes", align_bytes=64)
         w_plane = keep.tile([P, N], U8, name="w_plane", align_bytes=64)
-        x_rows = xT.rearrange("(p t) c -> p t c", t=4)
+        x_rows = xT.rearrange("(p t) c -> p t c", t=PACK)
 
         def load_row(t, loads):
             raw = keep.tile([P, T], F32, name=f"raw{t}")
             c0 = 0
-            for width, on_scalar, on_gpsimd in loads:
-                nc.sync.dma_start(raw[:, c0 : c0 + width], x_rows[:, t, c0 : c0 + width])
-                c0 = c0 + width
+            for load in loads:
+                nc.sync.dma_start(raw[:, c0 : c0 + load[0]], x_rows[:, t, c0 : c0 + load[0]])
+                c0 = c0 + load[0]
             return raw
 
         nc.sync.dma_start(task_list[:], task)
@@ -55,33 +59,34 @@ def tile_picked_none_e_kernel(tc, xT, w1_words, w1_scales, scale, offs, task, ou
             nc.sync.dma_start(tables[m][:], scale[m * P : (m + 1) * P, :])
         pair_chunks = []
         c0 = 0
-        for i, (width, on_scalar, on_gpsimd) in enumerate(PAIR_LOADS):
-            chunk = keep.tile([P, 2, width], F32, name=f"x01_{i}")
-            nc.sync.dma_start(chunk[:], x_rows[:, 0:2, c0 : c0 + width])
+        for i, load in enumerate(PAIR_LOADS):
+            chunk = keep.tile([P, 2, load[0]], F32, name=f"x01_{i}")
+            nc.sync.dma_start(chunk[:], x_rows[:, 0:2, c0 : c0 + load[0]])
             pair_chunks.append(chunk)
-            c0 = c0 + width
+            c0 = c0 + load[0]
             if i == 0:
                 nc.sync.dma_start(token_list[:], offs)
         raw2 = load_row(2, ROW2_LOADS)
         raw3 = load_row(3, ROW3_LOADS)
+
         nc.vector.memset(w_plane[:].bitcast(I32), 0)
         nc.sync.dma_start(w_codes[:].bitcast(I32), w1_words[0].bitcast(I32))
-        for q in range(4):
+        for q in range(P // 32):
             nc.sync.dma_start(w_plane[32 * q : 32 * q + 4, :].bitcast(I32), w1_scales[0, 4 * q : 4 * q + 4, :].bitcast(I32))
 
         def entries(i):
             return token_list[:, i * PIECE // LANES : (i + 1) * PIECE // LANES]
 
-        def gpsimd_cast(dst, src):
-            nc.gpsimd.tensor_scalar(dst, src, 1.0, 0.0, MULT, mybir.AluOpType.add)
+        def gpsimd_round(dst, src):
+            nc.gpsimd.tensor_scalar(dst, src, 1.0, 0.0, MULT, ADD)
 
         def shares(width, on_scalar, on_gpsimd):
             cuts = [0, on_scalar, on_scalar + on_gpsimd, width]
-            calls = [nc.scalar.copy, gpsimd_cast, nc.vector.tensor_copy]
-            return [(calls[e], cuts[e], cuts[e + 1]) for e in range(3) if cuts[e] < cuts[e + 1]]
+            calls = [nc.scalar.copy, gpsimd_round, nc.vector.tensor_copy]
+            return [(calls[e], cuts[e], cuts[e + 1]) for e in range(len(calls)) if cuts[e] < cuts[e + 1]]
 
         gains = keep.tile([P, M_TILES, S], F32, name="gains")
-        woven = [keep.tile([P, PIECE, 4], BF16, name=f"woven{i}", align_bytes=64) for i in range(COUNT)]
+        woven = [keep.tile([P, PIECE, PACK], BF16, name=f"woven{i}", align_bytes=64) for i in range(COUNT)]
 
         for m in range(M_TILES):
             for j0 in range(0, S, TASK_PIECE):
@@ -96,12 +101,12 @@ def tile_picked_none_e_kernel(tc, xT, w1_words, w1_scales, scale, offs, task, ou
             for call, a, b in shares(*load):
                 call(pairs[:, c0 + a : c0 + b, :], chunk[:, :, a:b].rearrange("p e c -> p c e"))
             c0 = c0 + load[0]
-        pair_words = pairs[:].rearrange("p t e -> p (t e)").bitcast(U32)
+        pair_words = pairs[:].rearrange("p c e -> p (c e)").bitcast(U32)
         for i in range(COUNT):
-            words = woven[i][:].rearrange("p n t -> p (n t)").bitcast(U32).rearrange("p (n u) -> p n u", u=2)
-            nc.vector.tensor_copy(words[:, :, 0], pair_words.indirect(entries(i)))
+            halves = woven[i][:].rearrange("p n t -> p (n t)").bitcast(U32).rearrange("p (n u) -> p n u", u=2)
+            nc.vector.tensor_copy(halves[:, :, 0], pair_words.indirect(entries(i)))
 
-        def single_row(t, raw, loads, on_vector):
+        def single_row(t, raw, loads):
             row = keep.tile([P, T], BF16, name=f"row{t}")
             c0 = 0
             for load in loads:
@@ -109,26 +114,24 @@ def tile_picked_none_e_kernel(tc, xT, w1_words, w1_scales, scale, offs, task, ou
                     call(row[:, c0 + a : c0 + b], raw[:, c0 + a : c0 + b])
                 c0 = c0 + load[0]
             for i in range(COUNT):
-                if i in on_vector:
+                if i == VECTOR_PIECE:
                     nc.vector.tensor_copy(woven[i][:, :, t], raw[:].indirect(entries(i)))
                 else:
                     nc.scalar.activation(woven[i][:, :, t], row[:].indirect(entries(i)), COPY)
 
-        single_row(2, raw2, ROW2_LOADS, ROW2_ON_VECTOR)
-        single_row(3, raw3, ROW3_LOADS, ROW3_ON_VECTOR)
+        single_row(2, raw2, ROW2_LOADS)
+        single_row(3, raw3, ROW3_LOADS)
 
         planes = [keep.tile([P, PIECE], U8, name=f"plane{i}", align_bytes=64) for i in range(COUNT)]
-        split = (0, COUNT - 1)
-        accs = []
+        banks = []
         for i in range(COUNT):
-            if i in split:
-                accs.append([psum.tile([P, PIECE], F32, name=f"acc{i}_{m}")[:] for m in range(M_TILES)])
+            if i in BY_BLOCK:
+                banks.append([psum.tile([P, PIECE], F32, name=f"acc{i}_{m}") for m in range(M_TILES)])
             else:
-                both = psum.tile([P, M_TILES, PIECE], F32, name=f"acc{i}")
-                accs.append([both[:, m, :] for m in range(M_TILES)] + [both[:]])
+                banks.append([psum.tile([P, M_TILES, PIECE], F32, name=f"acc{i}")])
 
         def multiply(i):
-            codes = keep.tile([P, PIECE], U32, name=f"codes{i}", tag=f"codes{i % 2}", align_bytes=64)
+            codes = keep.tile([P, PIECE], U32, name=f"codes{i}", tag=f"codes{i % CODE_BUFFERS}", align_bytes=64)
             nc.vector.quantize_mx(
                 out=codes[:].bitcast(FP8X4),
                 scales=planes[i][:],
@@ -136,7 +139,7 @@ def tile_picked_none_e_kernel(tc, xT, w1_words, w1_scales, scale, offs, task, ou
             )
             for m in range(M_TILES):
                 nc.tensor.matmul_mx(
-                    out=accs[i][m],
+                    out=banks[i][m][:] if i in BY_BLOCK else banks[i][0][:, m, :],
                     lhsT=w_codes[:, 2 * P * m : 2 * P * (m + 1)].bitcast(FP4X4),
                     lhsT_scale=w_plane[:, P * m : P * (m + 1)],
                     rhs=codes[:].bitcast(FP8X4),
@@ -150,12 +153,12 @@ def tile_picked_none_e_kernel(tc, xT, w1_words, w1_scales, scale, offs, task, ou
         def finish(i):
             cols = slice(i * PIECE, (i + 1) * PIECE)
             result = keep.tile([P, M_TILES, PIECE], F32, name=f"result{i}")
-            if i in split:
+            if i in BY_BLOCK:
                 for m in range(M_TILES):
-                    nc.vector.tensor_tensor(result[:, m, :], accs[i][m], gains[:, m, cols], MULT)
+                    nc.vector.tensor_tensor(result[:, m, :], banks[i][m][:], gains[:, m, cols], MULT)
                     nc.sync.dma_start(out_rows[:, m, cols], result[:, m, :])
             else:
-                nc.vector.tensor_tensor(result[:], accs[i][M_TILES], gains[:, :, cols], MULT)
+                nc.vector.tensor_tensor(result[:], banks[i][0][:], gains[:, :, cols], MULT)
                 nc.sync.dma_start(out_rows[:, :, cols], result[:])
 
         multiply(0)

@@ -27,8 +27,8 @@ TASK_PIECE = 512
 CODE_BUFFERS = 2
 
 PAIR_LOADS = [(1024, 544, 480), (768, 288, 0), (256, 96, 0)]
-ROW2_LOADS = [(1024, 576, 448), (512, 256, 256), (512, 512, 0)]
-ROW3_LOADS = [(1024, 0, 1024), (1024, 0, 0)]
+ROW2_LOADS = [(1024, 576, 448), (768, 416, 352), (256, 256, 0)]
+ROW3_LOADS = [(896, 0, 896), (1152, 0, 0)]
 VECTOR_PIECE = 0
 BY_BLOCK = (0, COUNT - 2, COUNT - 1)
 
@@ -64,8 +64,7 @@ def tile_picked_none_e_kernel(tc, xT, w1_words, w1_scales, scale, offs, task, ou
             nc.sync.dma_start(chunk[:], x_rows[:, 0:2, c0 : c0 + load[0]])
             pair_chunks.append(chunk)
             c0 = c0 + load[0]
-            if i == 0:
-                nc.sync.dma_start(token_list[:], offs)
+        nc.sync.dma_start(token_list[:], offs)
         raw2 = load_row(2, ROW2_LOADS)
         raw3 = load_row(3, ROW3_LOADS)
 

@@ -30,6 +30,7 @@ PAIR_LOADS = [(1024, 544, 480), (768, 288, 0), (256, 96, 0)]
 ROW2_LOADS = [(1024, 576, 448), (768, 416, 352), (256, 256, 0)]
 ROW3_LOADS = [(896, 0, 896), (1152, 0, 0)]
 VECTOR_PIECE = 0
+COPIED_PIECE = 3
 BY_BLOCK = (0, COUNT - 2, COUNT - 1)
 
 
@@ -101,9 +102,15 @@ def tile_picked_none_e_kernel(tc, xT, w1_words, w1_scales, scale, offs, task, ou
                 call(pairs[:, c0 + a : c0 + b, :], chunk[:, :, a:b].rearrange("p e c -> p c e"))
             c0 = c0 + load[0]
         pair_words = pairs[:].rearrange("p c e -> p (c e)").bitcast(U32)
+        apart = keep.tile([P, 2, PIECE, 2], BF16, name="apart")
+        apart_words = apart[:].rearrange("p u n e -> p u (n e)").bitcast(U32)
+
+        def words(i):
+            return woven[i][:].rearrange("p n t -> p (n t)").bitcast(U32).rearrange("p (n u) -> p n u", u=2)
+
         for i in range(COUNT):
-            halves = woven[i][:].rearrange("p n t -> p (n t)").bitcast(U32).rearrange("p (n u) -> p n u", u=2)
-            nc.vector.tensor_copy(halves[:, :, 0], pair_words.indirect(entries(i)))
+            dst = apart_words[:, 0, :] if i == COPIED_PIECE else words(i)[:, :, 0]
+            nc.vector.tensor_copy(dst, pair_words.indirect(entries(i)))
 
         def single_row(t, raw, loads):
             row = keep.tile([P, T], BF16, name=f"row{t}")
@@ -112,14 +119,17 @@ def tile_picked_none_e_kernel(tc, xT, w1_words, w1_scales, scale, offs, task, ou
                 for call, a, b in shares(*load):
                     call(row[:, c0 + a : c0 + b], raw[:, c0 + a : c0 + b])
                 c0 = c0 + load[0]
-            for i in range(COUNT):
+            for i in (0, 1, COPIED_PIECE, 2):
                 if i == VECTOR_PIECE:
                     nc.vector.tensor_copy(woven[i][:, :, t], raw[:].indirect(entries(i)))
+                elif i == COPIED_PIECE:
+                    nc.scalar.activation(apart[:, 1, :, t - 2], row[:].indirect(entries(i)), COPY)
                 else:
                     nc.scalar.activation(woven[i][:, :, t], row[:].indirect(entries(i)), COPY)
 
         single_row(2, raw2, ROW2_LOADS)
         single_row(3, raw3, ROW3_LOADS)
+        nc.scalar.copy(words(COPIED_PIECE), apart_words.rearrange("p u n -> p n u"))
 
         planes = [keep.tile([P, PIECE], U8, name=f"plane{i}", align_bytes=64) for i in range(COUNT)]
         banks = []

@@ -30,7 +30,7 @@ PAIR_LOADS = [(1024, 544, 480), (768, 288, 0), (256, 96, 0)]
 ROW2_LOADS = [(1024, 576, 448), (768, 416, 352), (256, 256, 0)]
 ROW3_LOADS = [(896, 0, 896), (1152, 0, 0)]
 VECTOR_PIECE = 0
-COPIED_PIECE = 3
+COPIED_PIECE = 2
 BY_BLOCK = (0, COUNT - 2, COUNT - 1)
 
 
@@ -119,7 +119,7 @@ def tile_picked_none_e_kernel(tc, xT, w1_words, w1_scales, scale, offs, task, ou
                 for call, a, b in shares(*load):
                     call(row[:, c0 + a : c0 + b], raw[:, c0 + a : c0 + b])
                 c0 = c0 + load[0]
-            for i in (0, 1, COPIED_PIECE, 2):
+            for i in range(COUNT):
                 if i == VECTOR_PIECE:
                     nc.vector.tensor_copy(woven[i][:, :, t], raw[:].indirect(entries(i)))
                 elif i == COPIED_PIECE:
@@ -129,7 +129,6 @@ def tile_picked_none_e_kernel(tc, xT, w1_words, w1_scales, scale, offs, task, ou
 
         single_row(2, raw2, ROW2_LOADS)
         single_row(3, raw3, ROW3_LOADS)
-        nc.scalar.copy(words(COPIED_PIECE), apart_words.rearrange("p u n -> p n u"))
 
         planes = [keep.tile([P, PIECE], U8, name=f"plane{i}", align_bytes=64) for i in range(COUNT)]
         banks = []
@@ -173,5 +172,7 @@ def tile_picked_none_e_kernel(tc, xT, w1_words, w1_scales, scale, offs, task, ou
         multiply(0)
         for i in range(1, COUNT):
             multiply(i)
+            if i + 1 == COPIED_PIECE:
+                nc.vector.tensor_copy(words(COPIED_PIECE), apart_words.rearrange("p u n -> p n u"))
             finish(i - 1)
         finish(COUNT - 1)

@@ -26,11 +26,13 @@ COUNT = S // PIECE
 TASK_PIECE = 512
 CODE_BUFFERS = 2
 
-PAIR_LOADS = [(1024, 544, 480), (768, 288, 0), (256, 96, 0)]
-ROW2_LOADS = [(1024, 576, 448), (768, 416, 352), (256, 256, 0)]
-ROW3_LOADS = [(896, 0, 896), (1152, 0, 0)]
-VECTOR_PIECE = 0
-COPIED_PIECE = 2
+ROW_LOADS = [
+    [(1024, 320, 0), (768, 256, 0), (256, 0, 0)],
+    [(768, 0, 768), (768, 384, 384), (512, 512, 0)],
+    [(640, 0, 640), (896, 128, 768), (512, 512, 0)],
+    [(640, 0, 640), (896, 0, 0), (512, 0, 0)],
+]
+VECTOR_PIECES = [(0,), (0,), (0, 1), (0,)]
 BY_BLOCK = (0, COUNT - 2, COUNT - 1)
 
 
@@ -46,28 +48,25 @@ def tile_picked_none_e_kernel(tc, xT, w1_words, w1_scales, scale, offs, task, ou
         w_codes = keep.tile([P, 2 * N], U8, name="w_codes", align_bytes=64)
         w_plane = keep.tile([P, N], U8, name="w_plane", align_bytes=64)
         x_rows = xT.rearrange("(p t) c -> p t c", t=PACK)
+        raws = [keep.tile([P, T], F32, name=f"raw{t}") for t in range(PACK)]
 
-        def load_row(t, loads):
-            raw = keep.tile([P, T], F32, name=f"raw{t}")
+        def load_row(t):
             c0 = 0
-            for load in loads:
-                nc.sync.dma_start(raw[:, c0 : c0 + load[0]], x_rows[:, t, c0 : c0 + load[0]])
+            for load in ROW_LOADS[t]:
+                nc.sync.dma_start(raws[t][:, c0 : c0 + load[0]], x_rows[:, t, c0 : c0 + load[0]])
                 c0 = c0 + load[0]
-            return raw
 
-        nc.sync.dma_start(task_list[:], task)
-        for m in range(M_TILES):
+        def load_table(m):
             nc.sync.dma_start(tables[m][:], scale[m * P : (m + 1) * P, :])
-        pair_chunks = []
-        c0 = 0
-        for i, load in enumerate(PAIR_LOADS):
-            chunk = keep.tile([P, 2, load[0]], F32, name=f"x01_{i}")
-            nc.sync.dma_start(chunk[:], x_rows[:, 0:2, c0 : c0 + load[0]])
-            pair_chunks.append(chunk)
-            c0 = c0 + load[0]
+
+        load_row(0)
         nc.sync.dma_start(token_list[:], offs)
-        raw2 = load_row(2, ROW2_LOADS)
-        raw3 = load_row(3, ROW3_LOADS)
+        nc.sync.dma_start(task_list[:], task)
+        load_table(0)
+        load_row(1)
+        load_table(1)
+        load_row(2)
+        load_row(3)
 
         nc.vector.memset(w_plane[:].bitcast(I32), 0)
         nc.sync.dma_start(w_codes[:].bitcast(I32), w1_words[0].bitcast(I32))
@@ -88,47 +87,32 @@ def tile_picked_none_e_kernel(tc, xT, w1_words, w1_scales, scale, offs, task, ou
         gains = keep.tile([P, M_TILES, S], F32, name="gains")
         woven = [keep.tile([P, PIECE, PACK], BF16, name=f"woven{i}", align_bytes=64) for i in range(COUNT)]
 
-        for m in range(M_TILES):
+        def gather_gains(m):
             for j0 in range(0, S, TASK_PIECE):
                 nc.vector.tensor_copy(
                     gains[:, m, j0 : j0 + TASK_PIECE],
                     tables[m][:].indirect(task_list[:, j0 // LANES : (j0 + TASK_PIECE) // LANES]),
                 )
 
-        pairs = keep.tile([P, T, 2], BF16, name="pairs")
-        c0 = 0
-        for load, chunk in zip(PAIR_LOADS, pair_chunks):
-            for call, a, b in shares(*load):
-                call(pairs[:, c0 + a : c0 + b, :], chunk[:, :, a:b].rearrange("p e c -> p c e"))
-            c0 = c0 + load[0]
-        pair_words = pairs[:].rearrange("p c e -> p (c e)").bitcast(U32)
-        apart = keep.tile([P, 2, PIECE, 2], BF16, name="apart")
-        apart_words = apart[:].rearrange("p u n e -> p u (n e)").bitcast(U32)
-
-        def words(i):
-            return woven[i][:].rearrange("p n t -> p (n t)").bitcast(U32).rearrange("p (n u) -> p n u", u=2)
-
-        for i in range(COUNT):
-            dst = apart_words[:, 0, :] if i == COPIED_PIECE else words(i)[:, :, 0]
-            nc.vector.tensor_copy(dst, pair_words.indirect(entries(i)))
-
-        def single_row(t, raw, loads):
+        def gather_row(t):
             row = keep.tile([P, T], BF16, name=f"row{t}")
             c0 = 0
-            for load in loads:
+            for load in ROW_LOADS[t]:
                 for call, a, b in shares(*load):
-                    call(row[:, c0 + a : c0 + b], raw[:, c0 + a : c0 + b])
+                    call(row[:, c0 + a : c0 + b], raws[t][:, c0 + a : c0 + b])
                 c0 = c0 + load[0]
             for i in range(COUNT):
-                if i == VECTOR_PIECE:
-                    nc.vector.tensor_copy(woven[i][:, :, t], raw[:].indirect(entries(i)))
-                elif i == COPIED_PIECE:
-                    nc.scalar.activation(apart[:, 1, :, t - 2], row[:].indirect(entries(i)), COPY)
+                if i in VECTOR_PIECES[t]:
+                    nc.vector.tensor_copy(woven[i][:, :, t], raws[t][:].indirect(entries(i)))
                 else:
                     nc.scalar.activation(woven[i][:, :, t], row[:].indirect(entries(i)), COPY)
 
-        single_row(2, raw2, ROW2_LOADS)
-        single_row(3, raw3, ROW3_LOADS)
+        gather_row(0)
+        gather_gains(0)
+        gather_row(1)
+        gather_gains(1)
+        gather_row(2)
+        gather_row(3)
 
         planes = [keep.tile([P, PIECE], U8, name=f"plane{i}", align_bytes=64) for i in range(COUNT)]
         banks = []
@@ -172,7 +156,5 @@ def tile_picked_none_e_kernel(tc, xT, w1_words, w1_scales, scale, offs, task, ou
         multiply(0)
         for i in range(1, COUNT):
             multiply(i)
-            if i + 1 == COPIED_PIECE:
-                nc.vector.tensor_copy(words(COPIED_PIECE), apart_words.rearrange("p u n -> p n u"))
             finish(i - 1)
         finish(COUNT - 1)

@@ -14,7 +14,6 @@ U8 = mybir.dt.uint8
 FP8X4 = mybir.dt.float8_e4m3fn_x4
 FP4X4 = mybir.dt.float4_e2m1fn_x4
 MULT = mybir.AluOpType.mult
-ADD = mybir.AluOpType.add
 COPY = mybir.ActivationFunctionType.Copy
 
 P = 128
@@ -23,17 +22,7 @@ LANES = 16
 M_TILES = N // P
 PIECE = 256
 COUNT = S // PIECE
-TASK_PIECE = 512
 CODE_BUFFERS = 2
-
-ROW_LOADS = [
-    [(1024, 320, 0), (768, 256, 0), (256, 0, 0)],
-    [(768, 0, 768), (768, 384, 384), (512, 512, 0)],
-    [(640, 0, 640), (896, 128, 768), (512, 512, 0)],
-    [(640, 0, 640), (896, 0, 0), (512, 0, 0)],
-]
-VECTOR_PIECES = [(0,), (0,), (0, 1), (0,)]
-BY_BLOCK = (0, COUNT - 2, COUNT - 1)
 
 
 def tile_picked_none_e_kernel(tc, xT, w1_words, w1_scales, scale, offs, task, out):
@@ -51,76 +40,60 @@ def tile_picked_none_e_kernel(tc, xT, w1_words, w1_scales, scale, offs, task, ou
         raws = [keep.tile([P, T], F32, name=f"raw{t}") for t in range(PACK)]
 
         def load_row(t):
-            c0 = 0
-            for load in ROW_LOADS[t]:
-                nc.sync.dma_start(raws[t][:, c0 : c0 + load[0]], x_rows[:, t, c0 : c0 + load[0]])
-                c0 = c0 + load[0]
+            nc.sync.dma_start(raws[t][:], x_rows[:, t, :])
 
         def load_table(m):
             nc.sync.dma_start(tables[m][:], scale[m * P : (m + 1) * P, :])
 
-        load_row(0)
-        nc.sync.dma_start(token_list[:], offs)
         nc.sync.dma_start(task_list[:], task)
         load_table(0)
-        load_row(1)
-        load_table(1)
-        load_row(2)
-        load_row(3)
+        nc.sync.dma_start(token_list[:], offs)
+        for t in range(PACK):
+            load_row(t)
 
         nc.vector.memset(w_plane[:].bitcast(I32), 0)
         nc.sync.dma_start(w_codes[:].bitcast(I32), w1_words[0].bitcast(I32))
         for q in range(P // 32):
             nc.sync.dma_start(w_plane[32 * q : 32 * q + 4, :].bitcast(I32), w1_scales[0, 4 * q : 4 * q + 4, :].bitcast(I32))
+        load_table(1)
 
-        def entries(i):
-            return token_list[:, i * PIECE // LANES : (i + 1) * PIECE // LANES]
+        def entries(the_list, i):
+            return the_list[:, i * PIECE // LANES : (i + 1) * PIECE // LANES]
 
-        def gpsimd_round(dst, src):
-            nc.gpsimd.tensor_scalar(dst, src, 1.0, 0.0, MULT, ADD)
-
-        def shares(width, on_scalar, on_gpsimd):
-            cuts = [0, on_scalar, on_scalar + on_gpsimd, width]
-            calls = [nc.scalar.copy, gpsimd_round, nc.vector.tensor_copy]
-            return [(calls[e], cuts[e], cuts[e + 1]) for e in range(len(calls)) if cuts[e] < cuts[e + 1]]
-
-        gains = keep.tile([P, M_TILES, S], F32, name="gains")
+        gains = [[keep.tile([P, PIECE], F32, name=f"gains{m}_{i}") for i in range(COUNT)] for m in range(M_TILES)]
         woven = [keep.tile([P, PIECE, PACK], BF16, name=f"woven{i}", align_bytes=64) for i in range(COUNT)]
 
-        def gather_gains(m):
-            for j0 in range(0, S, TASK_PIECE):
-                nc.vector.tensor_copy(
-                    gains[:, m, j0 : j0 + TASK_PIECE],
-                    tables[m][:].indirect(task_list[:, j0 // LANES : (j0 + TASK_PIECE) // LANES]),
-                )
+        def vector_gather(dst, window, offsets):
+            nc.vector.tensor_copy(dst, window.indirect(offsets))
+
+        def scalar_gather(dst, window, offsets):
+            nc.scalar.activation(dst, window.indirect(offsets), COPY)
+
+        for i in range(COUNT):
+            gather = scalar_gather if i == COUNT - 1 else vector_gather
+            gather(gains[0][i][:], tables[0][:], entries(task_list, i))
+
+        pairs = [[keep.tile([P, 2, PIECE], BF16, name=f"pair{u}_{i}") for i in range(1, COUNT)] for u in range(2)]
 
         def gather_row(t):
-            row = keep.tile([P, T], BF16, name=f"row{t}")
-            c0 = 0
-            for load in ROW_LOADS[t]:
-                for call, a, b in shares(*load):
-                    call(row[:, c0 + a : c0 + b], raws[t][:, c0 + a : c0 + b])
-                c0 = c0 + load[0]
-            for i in range(COUNT):
-                if i in VECTOR_PIECES[t]:
-                    nc.vector.tensor_copy(woven[i][:, :, t], raws[t][:].indirect(entries(i)))
-                else:
-                    nc.scalar.activation(woven[i][:, :, t], row[:].indirect(entries(i)), COPY)
+            vector_gather(woven[0][:, :, t], raws[t][:], entries(token_list, 0))
+            for i in range(1, COUNT):
+                scalar_gather(pairs[t // 2][i - 1][:, t % 2, :], raws[t][:], entries(token_list, i))
+
+        def weave(u, i):
+            nc.vector.tensor_copy(woven[i][:, :, 2 * u : 2 * u + 2], pairs[u][i - 1][:].rearrange("p t n -> p n t"))
 
         gather_row(0)
-        gather_gains(0)
         gather_row(1)
-        gather_gains(1)
+        for i in range(1, COUNT):
+            weave(0, i)
         gather_row(2)
         gather_row(3)
+        for i in range(COUNT):
+            scalar_gather(gains[1][i][:], tables[1][:], entries(task_list, i))
 
         planes = [keep.tile([P, PIECE], U8, name=f"plane{i}", align_bytes=64) for i in range(COUNT)]
-        banks = []
-        for i in range(COUNT):
-            if i in BY_BLOCK:
-                banks.append([psum.tile([P, PIECE], F32, name=f"acc{i}_{m}") for m in range(M_TILES)])
-            else:
-                banks.append([psum.tile([P, M_TILES, PIECE], F32, name=f"acc{i}")])
+        banks = [[psum.tile([P, PIECE], F32, name=f"acc{m}_{i}") for i in range(COUNT)] for m in range(M_TILES)]
 
         def multiply(i):
             codes = keep.tile([P, PIECE], U32, name=f"codes{i}", tag=f"codes{i % CODE_BUFFERS}", align_bytes=64)
@@ -131,7 +104,7 @@ def tile_picked_none_e_kernel(tc, xT, w1_words, w1_scales, scale, offs, task, ou
             )
             for m in range(M_TILES):
                 nc.tensor.matmul_mx(
-                    out=banks[i][m][:] if i in BY_BLOCK else banks[i][0][:, m, :],
+                    out=banks[m][i][:],
                     lhsT=w_codes[:, 2 * P * m : 2 * P * (m + 1)].bitcast(FP4X4),
                     lhsT_scale=w_plane[:, P * m : P * (m + 1)],
                     rhs=codes[:].bitcast(FP8X4),
@@ -140,21 +113,17 @@ def tile_picked_none_e_kernel(tc, xT, w1_words, w1_scales, scale, offs, task, ou
                     stop=True,
                 )
 
-        out_rows = out.rearrange("(m p) j -> p m j", p=P)
-
-        def finish(i):
-            cols = slice(i * PIECE, (i + 1) * PIECE)
-            result = keep.tile([P, M_TILES, PIECE], F32, name=f"result{i}")
-            if i in BY_BLOCK:
-                for m in range(M_TILES):
-                    nc.vector.tensor_tensor(result[:, m, :], banks[i][m][:], gains[:, m, cols], MULT)
-                    nc.sync.dma_start(out_rows[:, m, cols], result[:, m, :])
-            else:
-                nc.vector.tensor_tensor(result[:], banks[i][0][:], gains[:, :, cols], MULT)
-                nc.sync.dma_start(out_rows[:, :, cols], result[:])
+        def finish(m, i):
+            result = keep.tile([P, PIECE], F32, name=f"result{m}_{i}")
+            nc.vector.tensor_tensor(result[:], banks[m][i][:], gains[m][i][:], MULT)
+            nc.sync.dma_start(out[m * P : (m + 1) * P, i * PIECE : (i + 1) * PIECE], result[:])
 
         multiply(0)
         for i in range(1, COUNT):
+            weave(1, i)
             multiply(i)
-            finish(i - 1)
-        finish(COUNT - 1)
+            finish(0, i - 1)
+        finish(1, 0)
+        finish(0, COUNT - 1)
+        for i in range(1, COUNT):
+            finish(1, i)

@@ -45,17 +45,18 @@ def tile_picked_none_e_kernel(tc, xT, w1_words, w1_scales, scale, offs, task, ou
         def load_table(m):
             nc.sync.dma_start(tables[m][:], scale[m * P : (m + 1) * P, :])
 
-        nc.sync.dma_start(task_list[:], task)
-        load_table(0)
+        load_row(0)
         nc.sync.dma_start(token_list[:], offs)
-        for t in range(PACK):
+        for t in range(1, PACK):
             load_row(t)
 
         nc.vector.memset(w_plane[:].bitcast(I32), 0)
         nc.sync.dma_start(w_codes[:].bitcast(I32), w1_words[0].bitcast(I32))
         for q in range(P // 32):
             nc.sync.dma_start(w_plane[32 * q : 32 * q + 4, :].bitcast(I32), w1_scales[0, 4 * q : 4 * q + 4, :].bitcast(I32))
-        load_table(1)
+        nc.sync.dma_start(task_list[:], task)
+        for m in range(M_TILES):
+            load_table(m)
 
         def entries(the_list, i):
             return the_list[:, i * PIECE // LANES : (i + 1) * PIECE // LANES]
@@ -69,16 +70,13 @@ def tile_picked_none_e_kernel(tc, xT, w1_words, w1_scales, scale, offs, task, ou
         def scalar_gather(dst, window, offsets):
             nc.scalar.activation(dst, window.indirect(offsets), COPY)
 
-        for i in range(COUNT):
-            gather = scalar_gather if i == COUNT - 1 else vector_gather
-            gather(gains[0][i][:], tables[0][:], entries(task_list, i))
-
         pairs = [[keep.tile([P, 2, PIECE], BF16, name=f"pair{u}_{i}") for i in range(1, COUNT)] for u in range(2)]
 
         def gather_row(t):
             vector_gather(woven[0][:, :, t], raws[t][:], entries(token_list, 0))
             for i in range(1, COUNT):
-                scalar_gather(pairs[t // 2][i - 1][:, t % 2, :], raws[t][:], entries(token_list, i))
+                gather = vector_gather if t == 0 and i < COUNT - 1 else scalar_gather
+                gather(pairs[t // 2][i - 1][:, t % 2, :], raws[t][:], entries(token_list, i))
 
         def weave(u, i):
             nc.vector.tensor_copy(woven[i][:, :, 2 * u : 2 * u + 2], pairs[u][i - 1][:].rearrange("p t n -> p n t"))
@@ -89,8 +87,9 @@ def tile_picked_none_e_kernel(tc, xT, w1_words, w1_scales, scale, offs, task, ou
             weave(0, i)
         gather_row(2)
         gather_row(3)
-        for i in range(COUNT):
-            scalar_gather(gains[1][i][:], tables[1][:], entries(task_list, i))
+        order = [(m, i) for m in range(M_TILES) for i in range(COUNT)]
+        for m, i in order[1:]:
+            scalar_gather(gains[m][i][:], tables[m][:], entries(task_list, i))
 
         planes = [keep.tile([P, PIECE], U8, name=f"plane{i}", align_bytes=64) for i in range(COUNT)]
         banks = [[psum.tile([P, PIECE], F32, name=f"acc{m}_{i}") for i in range(COUNT)] for m in range(M_TILES)]
@@ -119,11 +118,14 @@ def tile_picked_none_e_kernel(tc, xT, w1_words, w1_scales, scale, offs, task, ou
             nc.sync.dma_start(out[m * P : (m + 1) * P, i * PIECE : (i + 1) * PIECE], result[:])
 
         multiply(0)
-        for i in range(1, COUNT):
-            weave(1, i)
-            multiply(i)
-            finish(0, i - 1)
-        finish(1, 0)
-        finish(0, COUNT - 1)
-        for i in range(1, COUNT):
-            finish(1, i)
+        weave(1, 1)
+        multiply(1)
+        vector_gather(gains[0][0][:], tables[0][:], entries(task_list, 0))
+        finish(0, 0)
+        weave(1, 2)
+        multiply(2)
+        finish(0, 1)
+        weave(1, 3)
+        multiply(3)
+        for m, i in order[2:]:
+            finish(m, i)

@@ -22,6 +22,7 @@ LANES = 16
 M_TILES = N // P
 PIECE = 256
 COUNT = S // PIECE
+DIRECT = (1, 2)
 CODE_BUFFERS = 2
 
 
@@ -61,7 +62,7 @@ def tile_picked_none_e_kernel(tc, xT, w1_words, w1_scales, scale, offs, task, ou
         def entries(the_list, i):
             return the_list[:, i * PIECE // LANES : (i + 1) * PIECE // LANES]
 
-        gains = [[keep.tile([P, PIECE], F32, name=f"gains{m}_{i}") for i in range(COUNT)] for m in range(M_TILES)]
+        gains = [[None] * COUNT for m in range(M_TILES)]
         woven = [keep.tile([P, PIECE, PACK], BF16, name=f"woven{i}", align_bytes=64) for i in range(COUNT)]
 
         def vector_gather(dst, window, offsets):
@@ -70,16 +71,20 @@ def tile_picked_none_e_kernel(tc, xT, w1_words, w1_scales, scale, offs, task, ou
         def scalar_gather(dst, window, offsets):
             nc.scalar.activation(dst, window.indirect(offsets), COPY)
 
-        pairs = [[keep.tile([P, 2, PIECE], BF16, name=f"pair{u}_{i}") for i in range(1, COUNT)] for u in range(2)]
+        pairs = [
+            {i: keep.tile([P, 2, PIECE], BF16, name=f"pair{u}_{i}") for i in range(DIRECT[u], COUNT)}
+            for u in range(2)
+        ]
 
         def gather_row(t):
-            vector_gather(woven[0][:, :, t], raws[t][:], entries(token_list, 0))
-            for i in range(1, COUNT):
+            for i in range(DIRECT[t // 2]):
+                vector_gather(woven[i][:, :, t], raws[t][:], entries(token_list, i))
+            for i in range(DIRECT[t // 2], COUNT):
                 gather = vector_gather if t == 0 and i < COUNT - 1 else scalar_gather
-                gather(pairs[t // 2][i - 1][:, t % 2, :], raws[t][:], entries(token_list, i))
+                gather(pairs[t // 2][i][:, t % 2, :], raws[t][:], entries(token_list, i))
 
         def weave(u, i):
-            nc.vector.tensor_copy(woven[i][:, :, 2 * u : 2 * u + 2], pairs[u][i - 1][:].rearrange("p t n -> p n t"))
+            nc.vector.tensor_copy(woven[i][:, :, 2 * u : 2 * u + 2], pairs[u][i][:].rearrange("p t n -> p n t"))
 
         gather_row(0)
         gather_row(1)
@@ -87,9 +92,12 @@ def tile_picked_none_e_kernel(tc, xT, w1_words, w1_scales, scale, offs, task, ou
             weave(0, i)
         gather_row(2)
         gather_row(3)
-        order = [(m, i) for m in range(M_TILES) for i in range(COUNT)]
-        for m, i in order[1:]:
-            scalar_gather(gains[m][i][:], tables[m][:], entries(task_list, i))
+        def gather_gains(gather, m, i, tag):
+            gains[m][i] = keep.tile([P, PIECE], F32, name=f"gains{m}_{i}", tag=tag)
+            gather(gains[m][i][:], tables[m][:], entries(task_list, i))
+
+        for m, i in [(m, i) for m in range(M_TILES) for i in range(COUNT)][:-1]:
+            gather_gains(scalar_gather, m, i, f"gains{m}_{i}")
 
         planes = [keep.tile([P, PIECE], U8, name=f"plane{i}", align_bytes=64) for i in range(COUNT)]
         banks = [[psum.tile([P, PIECE], F32, name=f"acc{m}_{i}") for i in range(COUNT)] for m in range(M_TILES)]
@@ -118,14 +126,17 @@ def tile_picked_none_e_kernel(tc, xT, w1_words, w1_scales, scale, offs, task, ou
             nc.sync.dma_start(out[m * P : (m + 1) * P, i * PIECE : (i + 1) * PIECE], result[:])
 
         multiply(0)
-        weave(1, 1)
         multiply(1)
-        vector_gather(gains[0][0][:], tables[0][:], entries(task_list, 0))
-        finish(0, 0)
         weave(1, 2)
+        finish(0, 0)
         multiply(2)
-        finish(0, 1)
         weave(1, 3)
+        finish(0, 1)
         multiply(3)
-        for m, i in order[2:]:
-            finish(m, i)
+        finish(0, 2)
+        gather_gains(vector_gather, 1, 3, "gains0_1")
+        finish(0, 3)
+        finish(1, 0)
+        finish(1, 3)
+        finish(1, 1)
+        finish(1, 2)

@@ -50,14 +50,14 @@ def tile_picked_none_e_kernel(tc, xT, w1_words, w1_scales, scale, offs, task, ou
         nc.sync.dma_start(token_list[:], offs)
         for t in range(1, PACK):
             load_row(t)
+        nc.sync.dma_start(task_list[:], task)
+        load_table(0)
 
         nc.vector.memset(w_plane[:].bitcast(I32), 0)
         nc.sync.dma_start(w_codes[:].bitcast(I32), w1_words[0].bitcast(I32))
         for q in range(P // 32):
             nc.sync.dma_start(w_plane[32 * q : 32 * q + 4, :].bitcast(I32), w1_scales[0, 4 * q : 4 * q + 4, :].bitcast(I32))
-        nc.sync.dma_start(task_list[:], task)
-        for m in range(M_TILES):
-            load_table(m)
+        load_table(1)
 
         def entries(the_list, i):
             return the_list[:, i * PIECE // LANES : (i + 1) * PIECE // LANES]

@@ -92,12 +92,13 @@ def tile_picked_none_e_kernel(tc, xT, w1_words, w1_scales, scale, offs, task, ou
             weave(0, i)
         gather_row(2)
         gather_row(3)
-        def gather_gains(gather, m, i, tag):
-            gains[m][i] = keep.tile([P, PIECE], F32, name=f"gains{m}_{i}", tag=tag)
-            gather(gains[m][i][:], tables[m][:], entries(task_list, i))
+        def gather_gains(gather, m, i, c0=0, c1=PIECE):
+            offsets = entries(task_list, i)[:, c0 // LANES : c1 // LANES]
+            gather(gains[m][i][:, c0:c1], tables[m][:], offsets)
 
-        for m, i in [(m, i) for m in range(M_TILES) for i in range(COUNT)][:-1]:
-            gather_gains(scalar_gather, m, i, f"gains{m}_{i}")
+        for m, i in [(0, 0), (0, 1), (0, 2), (1, 0), (0, 3), (1, 1), (1, 2)]:
+            gains[m][i] = keep.tile([P, PIECE], F32, name=f"gains{m}_{i}")
+            gather_gains(scalar_gather, m, i)
 
         planes = [keep.tile([P, PIECE], U8, name=f"plane{i}", align_bytes=64) for i in range(COUNT)]
         banks = [[psum.tile([P, PIECE], F32, name=f"acc{m}_{i}") for i in range(COUNT)] for m in range(M_TILES)]
@@ -130,13 +131,15 @@ def tile_picked_none_e_kernel(tc, xT, w1_words, w1_scales, scale, offs, task, ou
         weave(1, 2)
         finish(0, 0)
         multiply(2)
-        weave(1, 3)
         finish(0, 1)
-        multiply(3)
+        weave(1, 3)
         finish(0, 2)
-        gather_gains(vector_gather, 1, 3, "gains0_1")
-        finish(0, 3)
+        multiply(3)
         finish(1, 0)
-        finish(1, 3)
+        gains[1][3] = keep.tile([P, PIECE], F32, name="gains1_3", tag="gains0_2")
+        gather_gains(vector_gather, 1, 3, 0, PIECE // 2)
+        gather_gains(scalar_gather, 1, 3, PIECE // 2, PIECE)
+        finish(0, 3)
         finish(1, 1)
         finish(1, 2)
+        finish(1, 3)

@@ -92,13 +92,19 @@ def tile_picked_none_e_kernel(tc, xT, w1_words, w1_scales, scale, offs, task, ou
             weave(0, i)
         gather_row(2)
         gather_row(3)
-        def gather_gains(gather, m, i, c0=0, c1=PIECE):
+        def parts(m, i):
+            if (m, i) == (M_TILES - 1, COUNT - 1):
+                return [(0, PIECE // 2), (PIECE // 2, PIECE)]
+            return [(0, PIECE)]
+
+        def gather_gains(gather, m, i, c0, c1):
             offsets = entries(task_list, i)[:, c0 // LANES : c1 // LANES]
             gather(gains[m][i][:, c0:c1], tables[m][:], offsets)
 
-        for m, i in [(0, 0), (0, 1), (0, 2), (1, 0), (0, 3), (1, 1), (1, 2)]:
+        for m, i in [(0, 0), (0, 1), (0, 2), (1, 0), (0, 3), (1, 1), (1, 2), (1, 3)]:
             gains[m][i] = keep.tile([P, PIECE], F32, name=f"gains{m}_{i}")
-            gather_gains(scalar_gather, m, i)
+            for c0, c1 in parts(m, i):
+                gather_gains(scalar_gather, m, i, c0, c1)
 
         planes = [keep.tile([P, PIECE], U8, name=f"plane{i}", align_bytes=64) for i in range(COUNT)]
         banks = [[psum.tile([P, PIECE], F32, name=f"acc{m}_{i}") for i in range(COUNT)] for m in range(M_TILES)]
@@ -123,8 +129,9 @@ def tile_picked_none_e_kernel(tc, xT, w1_words, w1_scales, scale, offs, task, ou
 
         def finish(m, i):
             result = keep.tile([P, PIECE], F32, name=f"result{m}_{i}")
-            nc.vector.tensor_tensor(result[:], banks[m][i][:], gains[m][i][:], MULT)
-            nc.sync.dma_start(out[m * P : (m + 1) * P, i * PIECE : (i + 1) * PIECE], result[:])
+            for c0, c1 in parts(m, i):
+                nc.vector.tensor_tensor(result[:, c0:c1], banks[m][i][:, c0:c1], gains[m][i][:, c0:c1], MULT)
+                nc.sync.dma_start(out[m * P : (m + 1) * P, i * PIECE + c0 : i * PIECE + c1], result[:, c0:c1])
 
         multiply(0)
         multiply(1)
@@ -136,9 +143,6 @@ def tile_picked_none_e_kernel(tc, xT, w1_words, w1_scales, scale, offs, task, ou
         finish(0, 2)
         multiply(3)
         finish(1, 0)
-        gains[1][3] = keep.tile([P, PIECE], F32, name="gains1_3", tag="gains0_2")
-        gather_gains(vector_gather, 1, 3, 0, PIECE // 2)
-        gather_gains(scalar_gather, 1, 3, PIECE // 2, PIECE)
         finish(0, 3)
         finish(1, 1)
         finish(1, 2)

@@ -23,7 +23,6 @@ M_TILES = N // P
 PIECE = 256
 COUNT = S // PIECE
 DIRECT = (1, 2)
-CODE_BUFFERS = 2
 
 
 def tile_picked_none_e_kernel(tc, xT, w1_words, w1_scales, scale, offs, task, out):
@@ -101,31 +100,35 @@ def tile_picked_none_e_kernel(tc, xT, w1_words, w1_scales, scale, offs, task, ou
             offsets = entries(task_list, i)[:, c0 // LANES : c1 // LANES]
             gather(gains[m][i][:, c0:c1], tables[m][:], offsets)
 
-        for m, i in [(0, 0), (0, 1), (0, 2), (1, 0), (0, 3), (1, 1), (1, 2), (1, 3)]:
+        for m, i in [(m, i) for m in range(M_TILES) for i in range(COUNT)]:
             gains[m][i] = keep.tile([P, PIECE], F32, name=f"gains{m}_{i}")
             for c0, c1 in parts(m, i):
                 gather_gains(scalar_gather, m, i, c0, c1)
 
         planes = [keep.tile([P, PIECE], U8, name=f"plane{i}", align_bytes=64) for i in range(COUNT)]
-        banks = [[psum.tile([P, PIECE], F32, name=f"acc{m}_{i}") for i in range(COUNT)] for m in range(M_TILES)]
+        banks = [[None] * COUNT for m in range(M_TILES)]
 
-        def multiply(i):
-            codes = keep.tile([P, PIECE], U32, name=f"codes{i}", tag=f"codes{i % CODE_BUFFERS}", align_bytes=64)
+        codes = [None] * COUNT
+
+        def quantise(i):
+            codes[i] = keep.tile([P, PIECE], U32, name=f"codes{i}", tag=f"codes{i % 2}", align_bytes=64)
             nc.vector.quantize_mx(
-                out=codes[:].bitcast(FP8X4),
+                out=codes[i][:].bitcast(FP8X4),
                 scales=planes[i][:],
                 in_=woven[i][:].rearrange("p n t -> p (n t)"),
             )
-            for m in range(M_TILES):
-                nc.tensor.matmul_mx(
-                    out=banks[m][i][:],
-                    lhsT=w_codes[:, 2 * P * m : 2 * P * (m + 1)].bitcast(FP4X4),
-                    lhsT_scale=w_plane[:, P * m : P * (m + 1)],
-                    rhs=codes[:].bitcast(FP8X4),
-                    rhs_scale=planes[i][:],
-                    start=True,
-                    stop=True,
-                )
+
+        def multiply(m, i, bank):
+            banks[m][i] = psum.tile([P, PIECE], F32, name=f"acc{m}_{i}", tag=bank)
+            nc.tensor.matmul_mx(
+                out=banks[m][i][:],
+                lhsT=w_codes[:, 2 * P * m : 2 * P * (m + 1)].bitcast(FP4X4),
+                lhsT_scale=w_plane[:, P * m : P * (m + 1)],
+                rhs=codes[i][:].bitcast(FP8X4),
+                rhs_scale=planes[i][:],
+                start=True,
+                stop=True,
+            )
 
         def finish(m, i):
             result = keep.tile([P, PIECE], F32, name=f"result{m}_{i}")
@@ -133,17 +136,19 @@ def tile_picked_none_e_kernel(tc, xT, w1_words, w1_scales, scale, offs, task, ou
                 nc.vector.tensor_tensor(result[:, c0:c1], banks[m][i][:, c0:c1], gains[m][i][:, c0:c1], MULT)
                 nc.sync.dma_start(out[m * P : (m + 1) * P, i * PIECE + c0 : i * PIECE + c1], result[:, c0:c1])
 
-        multiply(0)
-        multiply(1)
+        for i in range(2):
+            quantise(i)
+            for m in range(M_TILES):
+                multiply(m, i, f"bank{m}_{i}")
         weave(1, 2)
-        finish(0, 0)
-        multiply(2)
-        finish(0, 1)
         weave(1, 3)
-        finish(0, 2)
-        multiply(3)
-        finish(1, 0)
-        finish(0, 3)
-        finish(1, 1)
-        finish(1, 2)
-        finish(1, 3)
+        finish(0, 0)
+        for i in range(2, COUNT):
+            quantise(i)
+            multiply(0, i, f"bank0_{i}")
+        for i in range(1, COUNT):
+            finish(0, i)
+        for i in range(2, COUNT):
+            multiply(1, i, f"bank0_{i - 1}")
+        for i in range(COUNT):
+            finish(1, i)

@@ -14,6 +14,7 @@ U8 = mybir.dt.uint8
 FP8X4 = mybir.dt.float8_e4m3fn_x4
 FP4X4 = mybir.dt.float4_e2m1fn_x4
 MULT = mybir.AluOpType.mult
+ADD = mybir.AluOpType.add
 COPY = mybir.ActivationFunctionType.Copy
 
 P = 128
@@ -70,20 +71,28 @@ def tile_picked_none_e_kernel(tc, xT, w1_words, w1_scales, scale, offs, task, ou
         def scalar_gather(dst, window, offsets):
             nc.scalar.activation(dst, window.indirect(offsets), COPY)
 
+        HALF = PIECE // 2
+        SHARED = 2
+        start = [HALF if i == SHARED else 0 for i in range(COUNT)]
+        quad = keep.tile([P, PACK, HALF], BF16, name="quad")
         pairs = [
-            {i: keep.tile([P, 2, PIECE], BF16, name=f"pair{u}_{i}") for i in range(DIRECT[u], COUNT)}
+            {i: keep.tile([P, 2, PIECE - start[i]], BF16, name=f"pair{u}_{i}") for i in range(DIRECT[u], COUNT)}
             for u in range(2)
         ]
 
         def gather_row(t):
             for i in range(DIRECT[t // 2]):
                 vector_gather(woven[i][:, :, t], raws[t][:], entries(token_list, i))
+            early = vector_gather if t == 0 else scalar_gather
+            early(quad[:, t, :], raws[t][:], entries(token_list, SHARED)[:, 0 : HALF // LANES])
             for i in range(DIRECT[t // 2], COUNT):
                 gather = vector_gather if t == 0 and i < COUNT - 1 else scalar_gather
-                gather(pairs[t // 2][i][:, t % 2, :], raws[t][:], entries(token_list, i))
+                gather(pairs[t // 2][i][:, t % 2, :], raws[t][:], entries(token_list, i)[:, start[i] // LANES :])
 
         def weave(u, i):
-            nc.vector.tensor_copy(woven[i][:, :, 2 * u : 2 * u + 2], pairs[u][i][:].rearrange("p t n -> p n t"))
+            nc.vector.tensor_copy(
+                woven[i][:, start[i] :, 2 * u : 2 * u + 2], pairs[u][i][:].rearrange("p t n -> p n t")
+            )
 
         gather_row(0)
         gather_row(1)
@@ -91,6 +100,8 @@ def tile_picked_none_e_kernel(tc, xT, w1_words, w1_scales, scale, offs, task, ou
             weave(0, i)
         gather_row(2)
         gather_row(3)
+        nc.gpsimd.tensor_scalar(woven[SHARED][:, 0:HALF, :], quad[:].rearrange("p t n -> p n t"), 1.0, 0.0, MULT, ADD)
+
         def parts(m, i):
             if (m, i) == (M_TILES - 1, COUNT - 1):
                 return [(0, PIECE // 2), (PIECE // 2, PIECE)]

@@ -62,7 +62,7 @@ def tile_picked_none_e_kernel(tc, xT, w1_words, w1_scales, scale, offs, task, ou
         def entries(the_list, i):
             return the_list[:, i * PIECE // LANES : (i + 1) * PIECE // LANES]
 
-        gains = [[None] * COUNT for m in range(M_TILES)]
+        gains = {}
         woven = [keep.tile([P, PIECE, PACK], BF16, name=f"woven{i}", align_bytes=64) for i in range(COUNT)]
 
         def vector_gather(dst, window, offsets):
@@ -76,8 +76,8 @@ def tile_picked_none_e_kernel(tc, xT, w1_words, w1_scales, scale, offs, task, ou
         start = [HALF if i == SHARED else 0 for i in range(COUNT)]
         quad = keep.tile([P, PACK, HALF], BF16, name="quad")
         pairs = [
-            {i: keep.tile([P, 2, PIECE - start[i]], BF16, name=f"pair{u}_{i}") for i in range(DIRECT[u], COUNT)}
-            for u in range(2)
+            {i: keep.tile([P, 2, PIECE - start[i]], BF16, name=f"pair0_{i}") for i in range(DIRECT[0], COUNT)},
+            keep.tile([P, 2, PIECE + HALF], BF16, name="pair1"),
         ]
 
         def gather_row(t):
@@ -85,14 +85,21 @@ def tile_picked_none_e_kernel(tc, xT, w1_words, w1_scales, scale, offs, task, ou
                 vector_gather(woven[i][:, :, t], raws[t][:], entries(token_list, i))
             early = vector_gather if t == 0 else scalar_gather
             early(quad[:, t, :], raws[t][:], entries(token_list, SHARED)[:, 0 : HALF // LANES])
-            for i in range(DIRECT[t // 2], COUNT):
+            if t >= 2:
+                scalar_gather(pairs[1][:, t % 2, :], raws[t][:], token_list[:, (SHARED * PIECE + HALF) // LANES :])
+                return
+            for i in range(DIRECT[0], COUNT):
                 gather = vector_gather if t == 0 and i < COUNT - 1 else scalar_gather
-                gather(pairs[t // 2][i][:, t % 2, :], raws[t][:], entries(token_list, i)[:, start[i] // LANES :])
+                gather(pairs[0][i][:, t % 2, :], raws[t][:], entries(token_list, i)[:, start[i] // LANES :])
 
         def weave(u, i):
-            nc.vector.tensor_copy(
-                woven[i][:, start[i] :, 2 * u : 2 * u + 2], pairs[u][i][:].rearrange("p t n -> p n t")
-            )
+            if u == 0:
+                src = pairs[0][i][:]
+            elif i == SHARED:
+                src = pairs[1][:, :, 0:HALF]
+            else:
+                src = pairs[1][:, :, HALF:]
+            nc.vector.tensor_copy(woven[i][:, start[i] :, 2 * u : 2 * u + 2], src.rearrange("p t n -> p n t"))
 
         gather_row(0)
         gather_row(1)
@@ -107,14 +114,13 @@ def tile_picked_none_e_kernel(tc, xT, w1_words, w1_scales, scale, offs, task, ou
                 return [(0, PIECE // 2), (PIECE // 2, PIECE)]
             return [(0, PIECE)]
 
-        def gather_gains(gather, m, i, c0, c1):
-            offsets = entries(task_list, i)[:, c0 // LANES : c1 // LANES]
-            gather(gains[m][i][:, c0:c1], tables[m][:], offsets)
-
-        for m, i in [(m, i) for m in range(M_TILES) for i in range(COUNT)]:
-            gains[m][i] = keep.tile([P, PIECE], F32, name=f"gains{m}_{i}")
-            for c0, c1 in parts(m, i):
-                gather_gains(scalar_gather, m, i, c0, c1)
+        spans = [[(0, 512), (512, S)], [(0, 512), (512, 768), (768, 896), (896, S)]]
+        for m in range(M_TILES):
+            for j0, j1 in spans[m]:
+                span = keep.tile([P, j1 - j0], F32, name=f"gains{m}_{j0}")
+                scalar_gather(span[:], tables[m][:], task_list[:, j0 // LANES : j1 // LANES])
+                for c0 in range(j0, j1, HALF):
+                    gains[(m, c0)] = (span, j0)
 
         planes = [keep.tile([P, PIECE], U8, name=f"plane{i}", align_bytes=64) for i in range(COUNT)]
         banks = [[None] * COUNT for m in range(M_TILES)]
@@ -144,7 +150,9 @@ def tile_picked_none_e_kernel(tc, xT, w1_words, w1_scales, scale, offs, task, ou
         def finish(m, i):
             result = keep.tile([P, PIECE], F32, name=f"result{m}_{i}")
             for c0, c1 in parts(m, i):
-                nc.vector.tensor_tensor(result[:, c0:c1], banks[m][i][:, c0:c1], gains[m][i][:, c0:c1], MULT)
+                span, j0 = gains[(m, i * PIECE + c0)]
+                gain = span[:, i * PIECE + c0 - j0 : i * PIECE + c1 - j0]
+                nc.vector.tensor_tensor(result[:, c0:c1], banks[m][i][:, c0:c1], gain, MULT)
                 nc.sync.dma_start(out[m * P : (m + 1) * P, i * PIECE + c0 : i * PIECE + c1], result[:, c0:c1])
 
         for i in range(2):

@@ -114,7 +114,7 @@ def tile_picked_none_e_kernel(tc, xT, w1_words, w1_scales, scale, offs, task, ou
                 return [(0, PIECE // 2), (PIECE // 2, PIECE)]
             return [(0, PIECE)]
 
-        spans = [[(0, 512), (512, S)], [(0, 512), (512, 768), (768, 896), (896, S)]]
+        spans = [[(0, 512), (512, S)], [(0, 256), (256, 512), (512, 768), (768, 896), (896, S)]]
         for m in range(M_TILES):
             for j0, j1 in spans[m]:
                 span = keep.tile([P, j1 - j0], F32, name=f"gains{m}_{j0}")

@@ -73,6 +73,7 @@ def tile_picked_none_e_kernel(tc, xT, w1_words, w1_scales, scale, offs, task, ou
 
         HALF = PIECE // 2
         SHARED = 2
+        EARLY = (1, 3, SHARED)
         start = [HALF if i == SHARED else 0 for i in range(COUNT)]
         quad = keep.tile([P, PACK, HALF], BF16, name="quad")
         pairs = [
@@ -83,14 +84,16 @@ def tile_picked_none_e_kernel(tc, xT, w1_words, w1_scales, scale, offs, task, ou
         def gather_row(t):
             for i in range(DIRECT[t // 2]):
                 vector_gather(woven[i][:, :, t], raws[t][:], entries(token_list, i))
-            early = vector_gather if t == 0 else scalar_gather
-            early(quad[:, t, :], raws[t][:], entries(token_list, SHARED)[:, 0 : HALF // LANES])
+            quad_entries = entries(token_list, SHARED)[:, 0 : HALF // LANES]
             if t >= 2:
+                scalar_gather(quad[:, t, :], raws[t][:], quad_entries)
                 scalar_gather(pairs[1][:, t % 2, :], raws[t][:], token_list[:, (SHARED * PIECE + HALF) // LANES :])
                 return
-            for i in range(DIRECT[0], COUNT):
+            for i in EARLY:
                 gather = vector_gather if t == 0 and i < COUNT - 1 else scalar_gather
                 gather(pairs[0][i][:, t % 2, :], raws[t][:], entries(token_list, i)[:, start[i] // LANES :])
+            early = vector_gather if t == 0 else scalar_gather
+            early(quad[:, t, :], raws[t][:], quad_entries)
 
         def weave(u, i):
             if u == 0:
@@ -103,7 +106,7 @@ def tile_picked_none_e_kernel(tc, xT, w1_words, w1_scales, scale, offs, task, ou
 
         gather_row(0)
         gather_row(1)
-        for i in range(1, COUNT):
+        for i in EARLY:
             weave(0, i)
         gather_row(2)
         gather_row(3)

@@ -24,6 +24,7 @@ M_TILES = N // P
 PIECE = 256
 COUNT = S // PIECE
 DIRECT = (1, 2)
+LEAD = (0, 0, 64, 0)
 
 
 def tile_picked_none_e_kernel(tc, xT, w1_words, w1_scales, scale, offs, task, out):
@@ -63,7 +64,7 @@ def tile_picked_none_e_kernel(tc, xT, w1_words, w1_scales, scale, offs, task, ou
             return the_list[:, i * PIECE // LANES : (i + 1) * PIECE // LANES]
 
         gains = {}
-        woven = [keep.tile([P, PIECE, PACK], BF16, name=f"woven{i}", align_bytes=64) for i in range(COUNT)]
+        woven = [keep.tile([P, PIECE + LEAD[i], PACK], BF16, name=f"woven{i}", align_bytes=1024)[:, LEAD[i] :, :] for i in range(COUNT)]
 
         def vector_gather(dst, window, offsets):
             nc.vector.tensor_copy(dst, window.indirect(offsets))
@@ -135,7 +136,7 @@ def tile_picked_none_e_kernel(tc, xT, w1_words, w1_scales, scale, offs, task, ou
             nc.vector.quantize_mx(
                 out=codes[i][:].bitcast(FP8X4),
                 scales=planes[i][:],
-                in_=woven[i][:].rearrange("p n t -> p (n t)"),
+                in_=woven[i].rearrange("p n t -> p (n t)"),
             )
 
         def multiply(m, i, bank):

@@ -25,21 +25,30 @@ PIECE = 256
 COUNT = S // PIECE
 DIRECT = (1, 2)
 LEAD = (0, 0, 64, 0)
+FAR = 65536
 
 
 def tile_picked_none_e_kernel(tc, xT, w1_words, w1_scales, scale, offs, task, out):
     nc = tc.nc
     with ExitStack() as ctx:
         keep = ctx.enter_context(tc.tile_pool(name="keep", bufs=1))
+        laid = ctx.enter_context(tc.tile_pool(name="laid", bufs=1))
         psum = ctx.enter_context(tc.psum_pool(name="psum", bufs=1))
+
+        used = [0, 0, 0, 0]
+
+        def place(region, shape, dtype, width, name):
+            offset = region * FAR + used[region]
+            used[region] = used[region] + width
+            return laid.tile(shape, dtype, name=name, offset=offset, align_bytes=1024)
 
         task_list = keep.tile([P, S // LANES], U16, name="task_list")
         token_list = keep.tile([P, S // LANES], U16, name="token_list")
-        tables = [keep.tile([P, U], F32, name=f"table{m}") for m in range(M_TILES)]
+        tables = [place(1, [P, U], F32, 4 * U, f"table{m}") for m in range(M_TILES)]
         w_codes = keep.tile([P, 2 * N], U8, name="w_codes", align_bytes=64)
         w_plane = keep.tile([P, N], U8, name="w_plane", align_bytes=64)
         x_rows = xT.rearrange("(p t) c -> p t c", t=PACK)
-        raws = [keep.tile([P, T], F32, name=f"raw{t}") for t in range(PACK)]
+        raws = [place(0, [P, T], F32, 4 * T, f"raw{t}") for t in range(PACK)]
 
         def load_row(t):
             nc.sync.dma_start(raws[t][:], x_rows[:, t, :])
@@ -64,7 +73,7 @@ def tile_picked_none_e_kernel(tc, xT, w1_words, w1_scales, scale, offs, task, ou
             return the_list[:, i * PIECE // LANES : (i + 1) * PIECE // LANES]
 
         gains = {}
-        woven = [keep.tile([P, PIECE + LEAD[i], PACK], BF16, name=f"woven{i}", align_bytes=1024)[:, LEAD[i] :, :] for i in range(COUNT)]
+        woven = [place(2, [P, PIECE + LEAD[i], PACK], BF16, 3072, f"woven{i}")[:, LEAD[i] :, :] for i in range(COUNT)]
 
         def vector_gather(dst, window, offsets):
             nc.vector.tensor_copy(dst, window.indirect(offsets))
@@ -76,10 +85,10 @@ def tile_picked_none_e_kernel(tc, xT, w1_words, w1_scales, scale, offs, task, ou
         SHARED = 2
         EARLY = (1, 3, SHARED)
         start = [HALF if i == SHARED else 0 for i in range(COUNT)]
-        quad = keep.tile([P, PACK, HALF], BF16, name="quad")
+        quad = place(3, [P, PACK, HALF], BF16, 1024, "quad")
         pairs = [
-            {i: keep.tile([P, 2, PIECE - start[i]], BF16, name=f"pair0_{i}") for i in range(DIRECT[0], COUNT)},
-            keep.tile([P, 2, PIECE + HALF], BF16, name="pair1"),
+            {i: place(3, [P, 2, PIECE - start[i]], BF16, 1024, f"pair0_{i}") for i in range(DIRECT[0], COUNT)},
+            place(3, [P, 2, PIECE + HALF], BF16, 2048, "pair1"),
         ]
 
         def gather_row(t):
@@ -118,10 +127,10 @@ def tile_picked_none_e_kernel(tc, xT, w1_words, w1_scales, scale, offs, task, ou
                 return [(0, PIECE // 2), (PIECE // 2, PIECE)]
             return [(0, PIECE)]
 
-        spans = [[(0, 512), (512, S)], [(0, 256), (256, 512), (512, 768), (768, 896), (896, S)]]
+        spans = [[(0, 512), (512, S)], [(0, 512), (512, 768), (768, 896), (896, S)]]
         for m in range(M_TILES):
             for j0, j1 in spans[m]:
-                span = keep.tile([P, j1 - j0], F32, name=f"gains{m}_{j0}")
+                span = place(3, [P, j1 - j0], F32, 2048, f"gains{m}_{j0}")
                 scalar_gather(span[:], tables[m][:], task_list[:, j0 // LANES : j1 // LANES])
                 for c0 in range(j0, j1, HALF):
                     gains[(m, c0)] = (span, j0)
@@ -152,7 +161,7 @@ def tile_picked_none_e_kernel(tc, xT, w1_words, w1_scales, scale, offs, task, ou
             )
 
         def finish(m, i):
-            result = keep.tile([P, PIECE], F32, name=f"result{m}_{i}")
+            result = place(2, [P, PIECE], F32, 1024, f"result{m}_{i}")
             for c0, c1 in parts(m, i):
                 span, j0 = gains[(m, i * PIECE + c0)]
                 gain = span[:, i * PIECE + c0 - j0 : i * PIECE + c1 - j0]

@@ -24,7 +24,7 @@ M_TILES = N // P
 PIECE = 256
 COUNT = S // PIECE
 DIRECT = (1, 2)
-LEAD = (0, 0, 64, 0)
+LEAD = (0, 0, 64, 64)
 FAR = 65536
 
 
@@ -108,10 +108,8 @@ def tile_picked_none_e_kernel(tc, xT, w1_words, w1_scales, scale, offs, task, ou
         def weave(u, i):
             if u == 0:
                 src = pairs[0][i][:]
-            elif i == SHARED:
-                src = pairs[1][:, :, 0:HALF]
             else:
-                src = pairs[1][:, :, HALF:]
+                src = pairs[1][:, :, 0:HALF]
             nc.vector.tensor_copy(woven[i][:, start[i] :, 2 * u : 2 * u + 2], src.rearrange("p t n -> p n t"))
 
         gather_row(0)
@@ -173,7 +171,9 @@ def tile_picked_none_e_kernel(tc, xT, w1_words, w1_scales, scale, offs, task, ou
             for m in range(M_TILES):
                 multiply(m, i, f"bank{m}_{i}")
         weave(1, 2)
-        weave(1, 3)
+        for h in range(2):
+            src = pairs[1][:, :, (h + 1) * HALF : (h + 2) * HALF]
+            nc.vector.tensor_copy(woven[3][:, h * HALF : (h + 1) * HALF, 2:4], src.rearrange("p t n -> p n t"))
         finish(0, 0)
         for i in range(2, COUNT):
             quantise(i)

@@ -139,7 +139,7 @@ def tile_picked_none_e_kernel(tc, xT, w1_words, w1_scales, scale, offs, task, ou
         codes = [None] * COUNT
 
         def quantise(i):
-            codes[i] = keep.tile([P, PIECE], U32, name=f"codes{i}", tag=f"codes{i % 2}", align_bytes=64)
+            codes[i] = keep.tile([P, PIECE], U32, name=f"codes{i}", align_bytes=64)
             nc.vector.quantize_mx(
                 out=codes[i][:].bitcast(FP8X4),
                 scales=planes[i][:],
@@ -174,11 +174,10 @@ def tile_picked_none_e_kernel(tc, xT, w1_words, w1_scales, scale, offs, task, ou
         for h in range(2):
             src = pairs[1][:, :, (h + 1) * HALF : (h + 2) * HALF]
             nc.vector.tensor_copy(woven[3][:, h * HALF : (h + 1) * HALF, 2:4], src.rearrange("p t n -> p n t"))
-        finish(0, 0)
         for i in range(2, COUNT):
             quantise(i)
             multiply(0, i, f"bank0_{i}")
-        for i in range(1, COUNT):
+        for i in range(COUNT):
             finish(0, i)
         for i in range(2, COUNT):
             multiply(1, i, f"bank0_{i - 1}")

@@ -26,6 +26,8 @@ COUNT = S // PIECE
 DIRECT = (1, 2)
 LEAD = (0, 0, 64, 64)
 FAR = 65536
+WHOLE = 96
+SPARE = 64
 
 
 def tile_picked_none_e_kernel(tc, xT, w1_words, w1_scales, scale, offs, task, out):
@@ -84,20 +86,21 @@ def tile_picked_none_e_kernel(tc, xT, w1_words, w1_scales, scale, offs, task, ou
         HALF = PIECE // 2
         SHARED = 2
         EARLY = (1, 3, SHARED)
-        start = [HALF if i == SHARED else 0 for i in range(COUNT)]
-        quad = place(3, [P, PACK, HALF], BF16, 1024, "quad")
+        start = [WHOLE if i == SHARED else 0 for i in range(COUNT)]
+        rest = PIECE - WHOLE
+        quad = place(3, [P, PACK, WHOLE], BF16, 1024, "quad")
         pairs = [
             {i: place(3, [P, 2, PIECE - start[i]], BF16, 1024, f"pair0_{i}") for i in range(DIRECT[0], COUNT)},
-            place(3, [P, 2, PIECE + HALF], BF16, 2048, "pair1"),
+            place(3, [P, 2, PIECE + rest], BF16, 2048, "pair1"),
         ]
 
         def gather_row(t):
             for i in range(DIRECT[t // 2]):
                 vector_gather(woven[i][:, :, t], raws[t][:], entries(token_list, i))
-            quad_entries = entries(token_list, SHARED)[:, 0 : HALF // LANES]
+            quad_entries = entries(token_list, SHARED)[:, 0 : WHOLE // LANES]
             if t >= 2:
                 scalar_gather(quad[:, t, :], raws[t][:], quad_entries)
-                scalar_gather(pairs[1][:, t % 2, :], raws[t][:], token_list[:, (SHARED * PIECE + HALF) // LANES :])
+                scalar_gather(pairs[1][:, t % 2, :], raws[t][:], token_list[:, (SHARED * PIECE + WHOLE) // LANES :])
                 return
             for i in EARLY:
                 gather = vector_gather if t == 0 and i < COUNT - 1 else scalar_gather
@@ -109,7 +112,7 @@ def tile_picked_none_e_kernel(tc, xT, w1_words, w1_scales, scale, offs, task, ou
             if u == 0:
                 src = pairs[0][i][:]
             else:
-                src = pairs[1][:, :, 0:HALF]
+                src = pairs[1][:, :, 0:rest]
             nc.vector.tensor_copy(woven[i][:, start[i] :, 2 * u : 2 * u + 2], src.rearrange("p t n -> p n t"))
 
         gather_row(0)
@@ -118,7 +121,7 @@ def tile_picked_none_e_kernel(tc, xT, w1_words, w1_scales, scale, offs, task, ou
             weave(0, i)
         gather_row(2)
         gather_row(3)
-        nc.gpsimd.tensor_scalar(woven[SHARED][:, 0:HALF, :], quad[:].rearrange("p t n -> p n t"), 1.0, 0.0, MULT, ADD)
+        nc.gpsimd.tensor_scalar(woven[SHARED][:, 0:WHOLE, :], quad[:].rearrange("p t n -> p n t"), 1.0, 0.0, MULT, ADD)
 
         def parts(m, i):
             if (m, i) == (M_TILES - 1, COUNT - 1):
@@ -129,7 +132,8 @@ def tile_picked_none_e_kernel(tc, xT, w1_words, w1_scales, scale, offs, task, ou
         for m in range(M_TILES):
             for j0, j1 in spans[m]:
                 span = place(3, [P, j1 - j0], F32, 2048, f"gains{m}_{j0}")
-                scalar_gather(span[:], tables[m][:], task_list[:, j0 // LANES : j1 // LANES])
+                last = j1 - SPARE if (m, j1) == (0, S) else j1
+                scalar_gather(span[:, 0 : last - j0], tables[m][:], task_list[:, j0 // LANES : last // LANES])
                 for c0 in range(j0, j1, HALF):
                     gains[(m, c0)] = (span, j0)
 
@@ -172,8 +176,10 @@ def tile_picked_none_e_kernel(tc, xT, w1_words, w1_scales, scale, offs, task, ou
                 multiply(m, i, f"bank{m}_{i}")
         weave(1, 2)
         for h in range(2):
-            src = pairs[1][:, :, (h + 1) * HALF : (h + 2) * HALF]
+            src = pairs[1][:, :, rest + h * HALF : rest + (h + 1) * HALF]
             nc.vector.tensor_copy(woven[3][:, h * HALF : (h + 1) * HALF, 2:4], src.rearrange("p t n -> p n t"))
+        span, j0 = gains[(0, S - HALF)]
+        vector_gather(span[:, S - SPARE - j0 :], tables[0][:], task_list[:, (S - SPARE) // LANES :])
         for i in range(2, COUNT):
             quantise(i)
             multiply(0, i, f"bank0_{i}")

@@ -27,7 +27,7 @@ DIRECT = (1, 2)
 LEAD = (0, 0, 64, 64)
 FAR = 65536
 WHOLE = 96
-SPARE = 64
+SPARE = 128
 
 
 def tile_picked_none_e_kernel(tc, xT, w1_words, w1_scales, scale, offs, task, out):
@@ -87,11 +87,10 @@ def tile_picked_none_e_kernel(tc, xT, w1_words, w1_scales, scale, offs, task, ou
         SHARED = 2
         EARLY = (1, 3, SHARED)
         start = [WHOLE if i == SHARED else 0 for i in range(COUNT)]
-        rest = PIECE - WHOLE
         quad = place(3, [P, PACK, WHOLE], BF16, 1024, "quad")
         pairs = [
             {i: place(3, [P, 2, PIECE - start[i]], BF16, 1024, f"pair0_{i}") for i in range(DIRECT[0], COUNT)},
-            place(3, [P, 2, PIECE + rest], BF16, 2048, "pair1"),
+            place(3, [P, 2, PIECE], BF16, 1024, "pair1"),
         ]
 
         def gather_row(t):
@@ -100,7 +99,8 @@ def tile_picked_none_e_kernel(tc, xT, w1_words, w1_scales, scale, offs, task, ou
             quad_entries = entries(token_list, SHARED)[:, 0 : WHOLE // LANES]
             if t >= 2:
                 scalar_gather(quad[:, t, :], raws[t][:], quad_entries)
-                scalar_gather(pairs[1][:, t % 2, :], raws[t][:], token_list[:, (SHARED * PIECE + WHOLE) // LANES :])
+                scalar_gather(pairs[1][:, t % 2, :], raws[t][:], entries(token_list, COUNT - 1))
+                scalar_gather(woven[SHARED][:, WHOLE:, t], raws[t][:], entries(token_list, SHARED)[:, WHOLE // LANES :])
                 return
             for i in EARLY:
                 gather = vector_gather if t == 0 and i < COUNT - 1 else scalar_gather
@@ -108,17 +108,13 @@ def tile_picked_none_e_kernel(tc, xT, w1_words, w1_scales, scale, offs, task, ou
             early = vector_gather if t == 0 else scalar_gather
             early(quad[:, t, :], raws[t][:], quad_entries)
 
-        def weave(u, i):
-            if u == 0:
-                src = pairs[0][i][:]
-            else:
-                src = pairs[1][:, :, 0:rest]
-            nc.vector.tensor_copy(woven[i][:, start[i] :, 2 * u : 2 * u + 2], src.rearrange("p t n -> p n t"))
+        def weave(i):
+            nc.vector.tensor_copy(woven[i][:, start[i] :, 0:2], pairs[0][i][:].rearrange("p t n -> p n t"))
 
         gather_row(0)
         gather_row(1)
         for i in EARLY:
-            weave(0, i)
+            weave(i)
         gather_row(2)
         gather_row(3)
         nc.gpsimd.tensor_scalar(woven[SHARED][:, 0:WHOLE, :], quad[:].rearrange("p t n -> p n t"), 1.0, 0.0, MULT, ADD)
@@ -174,15 +170,14 @@ def tile_picked_none_e_kernel(tc, xT, w1_words, w1_scales, scale, offs, task, ou
             quantise(i)
             for m in range(M_TILES):
                 multiply(m, i, f"bank{m}_{i}")
-        weave(1, 2)
         for h in range(2):
-            src = pairs[1][:, :, rest + h * HALF : rest + (h + 1) * HALF]
+            src = pairs[1][:, :, h * HALF : (h + 1) * HALF]
             nc.vector.tensor_copy(woven[3][:, h * HALF : (h + 1) * HALF, 2:4], src.rearrange("p t n -> p n t"))
-        span, j0 = gains[(0, S - HALF)]
-        vector_gather(span[:, S - SPARE - j0 :], tables[0][:], task_list[:, (S - SPARE) // LANES :])
         for i in range(2, COUNT):
             quantise(i)
             multiply(0, i, f"bank0_{i}")
+        span, j0 = gains[(0, S - HALF)]
+        vector_gather(span[:, S - SPARE - j0 :], tables[0][:], task_list[:, (S - SPARE) // LANES :])
         for i in range(COUNT):
             finish(0, i)
         for i in range(2, COUNT):

@@ -14,7 +14,6 @@ U8 = mybir.dt.uint8
 FP8X4 = mybir.dt.float8_e4m3fn_x4
 FP4X4 = mybir.dt.float4_e2m1fn_x4
 MULT = mybir.AluOpType.mult
-ADD = mybir.AluOpType.add
 COPY = mybir.ActivationFunctionType.Copy
 
 P = 128
@@ -24,10 +23,9 @@ M_TILES = N // P
 PIECE = 256
 COUNT = S // PIECE
 DIRECT = (1, 2)
-LEAD = (0, 0, 64, 64)
+LEAD = (0, 0, 0, 64)
 FAR = 65536
-WHOLE = 96
-SPARE = 128
+SPARE = 160
 
 
 def tile_picked_none_e_kernel(tc, xT, w1_words, w1_scales, scale, offs, task, out):
@@ -84,50 +82,34 @@ def tile_picked_none_e_kernel(tc, xT, w1_words, w1_scales, scale, offs, task, ou
             nc.scalar.activation(dst, window.indirect(offsets), COPY)
 
         HALF = PIECE // 2
-        SHARED = 2
-        EARLY = (1, 3, SHARED)
-        start = [WHOLE if i == SHARED else 0 for i in range(COUNT)]
-        quad = place(3, [P, PACK, WHOLE], BF16, 1024, "quad")
-        pairs = [
-            {i: place(3, [P, 2, PIECE - start[i]], BF16, 1024, f"pair0_{i}") for i in range(DIRECT[0], COUNT)},
-            place(3, [P, 2, PIECE], BF16, 1024, "pair1"),
-        ]
+        STEPPED = 2
+        LAST = COUNT - 1
+        pairs = [{i: place(3, [P, 2, PIECE], BF16, 1024, f"pair{u}_{i}") for i in range(DIRECT[u], COUNT) if i != STEPPED} for u in range(2)]
 
         def gather_row(t):
             for i in range(DIRECT[t // 2]):
                 vector_gather(woven[i][:, :, t], raws[t][:], entries(token_list, i))
-            quad_entries = entries(token_list, SHARED)[:, 0 : WHOLE // LANES]
-            if t >= 2:
-                scalar_gather(quad[:, t, :], raws[t][:], quad_entries)
-                scalar_gather(pairs[1][:, t % 2, :], raws[t][:], entries(token_list, COUNT - 1))
-                scalar_gather(woven[SHARED][:, WHOLE:, t], raws[t][:], entries(token_list, SHARED)[:, WHOLE // LANES :])
-                return
-            for i in EARLY:
-                gather = vector_gather if t == 0 and i < COUNT - 1 else scalar_gather
-                gather(pairs[0][i][:, t % 2, :], raws[t][:], entries(token_list, i)[:, start[i] // LANES :])
-            early = vector_gather if t == 0 else scalar_gather
-            early(quad[:, t, :], raws[t][:], quad_entries)
-
-        def weave(i):
-            nc.vector.tensor_copy(woven[i][:, start[i] :, 0:2], pairs[0][i][:].rearrange("p t n -> p n t"))
+            gather = vector_gather if t == 0 else scalar_gather
+            for i in pairs[t // 2]:
+                gather(pairs[t // 2][i][:, t % 2, :], raws[t][:], entries(token_list, i))
+            scalar_gather(woven[STEPPED][:, :, t], raws[t][:], entries(token_list, STEPPED))
 
         gather_row(0)
         gather_row(1)
-        for i in EARLY:
-            weave(i)
+        for i in pairs[0]:
+            nc.vector.tensor_copy(woven[i][:, :, 0:2], pairs[0][i][:].rearrange("p t n -> p n t"))
         gather_row(2)
         gather_row(3)
-        nc.gpsimd.tensor_scalar(woven[SHARED][:, 0:WHOLE, :], quad[:].rearrange("p t n -> p n t"), 1.0, 0.0, MULT, ADD)
 
         def parts(m, i):
             if (m, i) == (M_TILES - 1, COUNT - 1):
                 return [(0, PIECE // 2), (PIECE // 2, PIECE)]
             return [(0, PIECE)]
 
-        spans = [[(0, 512), (512, S)], [(0, 512), (512, 768), (768, 896), (896, S)]]
+        spans = [[(0, S)], [(0, 512), (512, 768), (768, 896), (896, S)]]
         for m in range(M_TILES):
             for j0, j1 in spans[m]:
-                span = place(3, [P, j1 - j0], F32, 2048, f"gains{m}_{j0}")
+                span = place(3, [P, j1 - j0], F32, 4096, f"gains{m}_{j0}")
                 last = j1 - SPARE if (m, j1) == (0, S) else j1
                 scalar_gather(span[:, 0 : last - j0], tables[m][:], task_list[:, j0 // LANES : last // LANES])
                 for c0 in range(j0, j1, HALF):
@@ -166,13 +148,15 @@ def tile_picked_none_e_kernel(tc, xT, w1_words, w1_scales, scale, offs, task, ou
                 nc.vector.tensor_tensor(result[:, c0:c1], banks[m][i][:, c0:c1], gain, MULT)
                 nc.sync.dma_start(out[m * P : (m + 1) * P, i * PIECE + c0 : i * PIECE + c1], result[:, c0:c1])
 
-        for i in range(2):
-            quantise(i)
-            for m in range(M_TILES):
-                multiply(m, i, f"bank{m}_{i}")
+        quantise(0)
+        for m in range(M_TILES):
+            multiply(m, 0, f"bank{m}_0")
         for h in range(2):
-            src = pairs[1][:, :, h * HALF : (h + 1) * HALF]
-            nc.vector.tensor_copy(woven[3][:, h * HALF : (h + 1) * HALF, 2:4], src.rearrange("p t n -> p n t"))
+            src = pairs[1][LAST][:, :, h * HALF : (h + 1) * HALF]
+            nc.vector.tensor_copy(woven[LAST][:, h * HALF : (h + 1) * HALF, 2:4], src.rearrange("p t n -> p n t"))
+        quantise(1)
+        for m in range(M_TILES):
+            multiply(m, 1, f"bank{m}_1")
         for i in range(2, COUNT):
             quantise(i)
             multiply(0, i, f"bank0_{i}")

@@ -69,6 +69,10 @@ def tile_picked_none_e_kernel(tc, xT, w1_words, w1_scales, scale, offs, task, ou
             nc.sync.dma_start(w_plane[32 * q : 32 * q + 4, :].bitcast(I32), w1_scales[0, 4 * q : 4 * q + 4, :].bitcast(I32))
         load_table(1)
 
+        idle = keep.tile([P, 2, 8], F32, name="idle")
+        nc.vector.memset(idle[:, 0, :], 0.0)
+        nc.scalar.activation(idle[:, 1, :], idle[:, 0, :], COPY)
+
         def entries(the_list, i):
             return the_list[:, i * PIECE // LANES : (i + 1) * PIECE // LANES]
 

from contextlib import ExitStack

import concourse.mybir as mybir

K, T, S, N, U = 512, 2048, 1024, 256, 1024
FLOPS = 2 * K * N * S

F32 = mybir.dt.float32
BF16 = mybir.dt.bfloat16
I32 = mybir.dt.int32
U32 = mybir.dt.uint32
U16 = mybir.dt.uint16
U8 = mybir.dt.uint8
FP8X4 = mybir.dt.float8_e4m3fn_x4
FP4X4 = mybir.dt.float4_e2m1fn_x4
MULT = mybir.AluOpType.mult
COPY = mybir.ActivationFunctionType.Copy

P = 128
PACK = 4
LANES = 16
M_TILES = N // P
PIECE = 256
COUNT = S // PIECE
DIRECT = (1, 2)
LEAD = (0, 0, 0, 64)
FAR = 65536
SPARE = 160


def tile_picked_none_e_kernel(tc, xT, w1_words, w1_scales, scale, offs, task, out):
    nc = tc.nc
    with ExitStack() as ctx:
        keep = ctx.enter_context(tc.tile_pool(name="keep", bufs=1))
        laid = ctx.enter_context(tc.tile_pool(name="laid", bufs=1))
        psum = ctx.enter_context(tc.psum_pool(name="psum", bufs=1))

        used = [0, 0, 0, 0]

        def place(region, shape, dtype, width, name):
            offset = region * FAR + used[region]
            used[region] = used[region] + width
            return laid.tile(shape, dtype, name=name, offset=offset, align_bytes=1024)

        task_list = keep.tile([P, S // LANES], U16, name="task_list")
        token_list = keep.tile([P, S // LANES], U16, name="token_list")
        tables = [place(1, [P, U], F32, 4 * U, f"table{m}") for m in range(M_TILES)]
        w_codes = keep.tile([P, 2 * N], U8, name="w_codes", align_bytes=64)
        w_plane = keep.tile([P, N], U8, name="w_plane", align_bytes=64)
        x_rows = xT.rearrange("(p t) c -> p t c", t=PACK)
        raws = [place(0, [P, T], F32, 4 * T, f"raw{t}") for t in range(PACK)]

        def load_row(t):
            nc.sync.dma_start(raws[t][:], x_rows[:, t, :])

        def load_table(m):
            nc.sync.dma_start(tables[m][:], scale[m * P : (m + 1) * P, :])

        load_row(0)
        nc.sync.dma_start(token_list[:], offs)
        for t in range(1, PACK):
            load_row(t)
        nc.sync.dma_start(task_list[:], task)
        load_table(0)

        nc.vector.memset(w_plane[:].bitcast(I32), 0)
        nc.sync.dma_start(w_codes[:].bitcast(I32), w1_words[0].bitcast(I32))
        for q in range(P // 32):
            nc.sync.dma_start(w_plane[32 * q : 32 * q + 4, :].bitcast(I32), w1_scales[0, 4 * q : 4 * q + 4, :].bitcast(I32))
        load_table(1)

        idle = keep.tile([P, 2, 8], F32, name="idle")
        nc.vector.memset(idle[:, 0, :], 0.0)
        nc.scalar.activation(idle[:, 1, :], idle[:, 0, :], COPY)

        def entries(the_list, i):
            return the_list[:, i * PIECE // LANES : (i + 1) * PIECE // LANES]

        gains = {}
        woven = [place(2, [P, PIECE + LEAD[i], PACK], BF16, 3072, f"woven{i}")[:, LEAD[i] :, :] for i in range(COUNT)]

        def vector_gather(dst, window, offsets):
            nc.vector.tensor_copy(dst, window.indirect(offsets))

        def scalar_gather(dst, window, offsets):
            nc.scalar.activation(dst, window.indirect(offsets), COPY)

        HALF = PIECE // 2
        STEPPED = 2
        LAST = COUNT - 1
        pairs = [{i: place(3, [P, 2, PIECE], BF16, 1024, f"pair{u}_{i}") for i in range(DIRECT[u], COUNT) if i != STEPPED} for u in range(2)]

        def gather_row(t):
            for i in range(DIRECT[t // 2]):
                vector_gather(woven[i][:, :, t], raws[t][:], entries(token_list, i))
            gather = vector_gather if t == 0 else scalar_gather
            for i in pairs[t // 2]:
                gather(pairs[t // 2][i][:, t % 2, :], raws[t][:], entries(token_list, i))
            scalar_gather(woven[STEPPED][:, :, t], raws[t][:], entries(token_list, STEPPED))

        gather_row(0)
        gather_row(1)
        for i in pairs[0]:
            nc.vector.tensor_copy(woven[i][:, :, 0:2], pairs[0][i][:].rearrange("p t n -> p n t"))
        gather_row(2)
        gather_row(3)

        def parts(m, i):
            if (m, i) == (M_TILES - 1, COUNT - 1):
                return [(0, PIECE // 2), (PIECE // 2, PIECE)]
            return [(0, PIECE)]

        spans = [[(0, S)], [(0, 512), (512, 768), (768, 896), (896, S)]]
        for m in range(M_TILES):
            for j0, j1 in spans[m]:
                span = place(3, [P, j1 - j0], F32, 4096, f"gains{m}_{j0}")
                last = j1 - SPARE if (m, j1) == (0, S) else j1
                scalar_gather(span[:, 0 : last - j0], tables[m][:], task_list[:, j0 // LANES : last // LANES])
                for c0 in range(j0, j1, HALF):
                    gains[(m, c0)] = (span, j0)

        planes = [keep.tile([P, PIECE], U8, name=f"plane{i}", align_bytes=64) for i in range(COUNT)]
        banks = [[None] * COUNT for m in range(M_TILES)]

        codes = [None] * COUNT

        def quantise(i):
            codes[i] = keep.tile([P, PIECE], U32, name=f"codes{i}", align_bytes=64)
            nc.vector.quantize_mx(
                out=codes[i][:].bitcast(FP8X4),
                scales=planes[i][:],
                in_=woven[i].rearrange("p n t -> p (n t)"),
            )

        def multiply(m, i, bank):
            banks[m][i] = psum.tile([P, PIECE], F32, name=f"acc{m}_{i}", tag=bank)
            nc.tensor.matmul_mx(
                out=banks[m][i][:],
                lhsT=w_codes[:, 2 * P * m : 2 * P * (m + 1)].bitcast(FP4X4),
                lhsT_scale=w_plane[:, P * m : P * (m + 1)],
                rhs=codes[i][:].bitcast(FP8X4),
                rhs_scale=planes[i][:],
                start=True,
                stop=True,
            )

        def finish(m, i):
            result = place(2, [P, PIECE], F32, 1024, f"result{m}_{i}")
            for c0, c1 in parts(m, i):
                span, j0 = gains[(m, i * PIECE + c0)]
                gain = span[:, i * PIECE + c0 - j0 : i * PIECE + c1 - j0]
                nc.vector.tensor_tensor(result[:, c0:c1], banks[m][i][:, c0:c1], gain, MULT)
                nc.sync.dma_start(out[m * P : (m + 1) * P, i * PIECE + c0 : i * PIECE + c1], result[:, c0:c1])

        quantise(0)
        for m in range(M_TILES):
            multiply(m, 0, f"bank{m}_0")
        for h in range(2):
            src = pairs[1][LAST][:, :, h * HALF : (h + 1) * HALF]
            nc.vector.tensor_copy(woven[LAST][:, h * HALF : (h + 1) * HALF, 2:4], src.rearrange("p t n -> p n t"))
        quantise(1)
        for m in range(M_TILES):
            multiply(m, 1, f"bank{m}_1")
        for i in range(2, COUNT):
            quantise(i)
            multiply(0, i, f"bank0_{i}")
        span, j0 = gains[(0, S - HALF)]
        vector_gather(span[:, S - SPARE - j0 :], tables[0][:], task_list[:, (S - SPARE) // LANES :])
        for i in range(COUNT):
            finish(0, i)
        for i in range(2, COUNT):
            multiply(1, i, f"bank0_{i - 1}")
        for i in range(COUNT):
            finish(1, i)
